import numpy as np, ml_dtypes
CORES = [24,25,26,27,28,29,30,31]
N = 8
import mx_ref
BF = ml_dtypes.bfloat16
def f(rng, *shape):
    return mx_ref.flush((rng.standard_normal(shape, dtype=np.float32) * np.exp2(rng.integers(-2, 3, shape[:-1] + (1,)))).astype(BF))
def wide(rng, *shape, cols=0):
    v = rng.standard_normal(shape, dtype=np.float32) * np.exp2(rng.integers(-12, 13, shape)).astype(np.float32)
    if cols: v *= np.repeat(np.exp2(rng.integers(-cols, cols + 1, shape[:-2] + (1, shape[-1] // 4))) * (rng.random(shape[:-2] + (1, shape[-1] // 4)) > 0.0625), 4, axis=-1).astype(np.float32)
    return mx_ref.flush(v.astype(BF))
T, NB, CH, BW = 512, 4, 64, 128
def scores(x, u):
    return np.stack([mx_ref.matmul(mx_ref.quantize(u[s]), mx_ref.quantize(x[s]))[0] for s in range(N)]) + np.float32(0.0)
def dealt(rng, d, place):
    v = d["x"].reshape(N, 128, T, 4).transpose(0, 2, 1, 3).reshape(N * T, 128, 4)
    g = np.argsort(-scores(d["x"], d["u"]).reshape(-1), kind="stable")
    e = np.stack([g[rng.permutation(place[s])] for s in range(N)])
    return np.ascontiguousarray(v[e].transpose(0, 2, 1, 3)).reshape(N, 128, 4 * T)
def setup_inputs(rng):
    u = np.zeros((N, 128, 512), BF); u[:, :, :4] = f(rng, 128, 4)
    return {"x": f(rng, N, 128, 4 * T), "u": u, "w": f(rng, N, 128, 512 * NB)}
def setup_inputs_ties(rng):
    d = setup_inputs(rng); d["u"][:, 64:] = 0; few = f(rng, 64, 24).reshape(64, 6, 4)
    for s in range(N):
        e = rng.permutation(np.concatenate([np.arange(6), rng.choice(6, T - 6, p=rng.dirichlet(np.ones(6)))]))
        d["x"][s, :64] = few[:, e].reshape(64, -1)
    return d
def setup_inputs_blocks(rng):
    d = setup_inputs(rng); d["x"] = dealt(rng, d, np.arange(N * T).reshape(N, T)[rng.permutation(N)]); return d
def setup_inputs_alternate(rng):
    d = setup_inputs(rng); d["x"] = dealt(rng, d, np.arange(N * T).reshape(T, N).T[rng.permutation(N)]); return d
def setup_inputs_zeros(rng):
    d = setup_inputs(rng); d["u"][:, 64:] = 0
    for s in rng.permutation(N)[:N // 2]: d["x"][s, :64] = 0
    return d
def setup_inputs_spread(rng):
    d = setup_inputs(rng); k = np.where(rng.permutation(N) < N // 2, np.float32(2.0 ** -20), np.float32(2.0 ** 7))
    d["x"] = mx_ref.flush((wide(rng, N, 128, 4 * T, cols=8).astype(np.float32) * k[:, None, None]).astype(BF))
    d["u"] = (d["u"].astype(np.float32) * np.float32(2 ** 24)).astype(BF); return d
def check_inputs(d):
    b = []; u = np.asarray(d["u"]).astype(np.float32)
    for r in range(N):
        if (u[r][:, 4:] != 0).any() or (u[r] != u[0]).any(): b.append("u")
    return b
def reference(x, u, w):
    score = scores(x, u)
    order = [np.argsort(-score[s], kind="stable") for s in range(N)]
    y = np.zeros((N, 128, T), np.float32); ids = np.zeros((N, 2, T), np.float32)
    for d in range(N):
        runs = [order[s][CH * d:CH * d + CH] for s in range(N)]
        rank = np.repeat(np.arange(N), CH); col = np.concatenate(runs)
        m = np.argsort(-score[rank, col], kind="stable")
        rank, col = rank[m], col[m]
        ids[d, 0], ids[d, 1] = rank, col
        t = np.ascontiguousarray(x.reshape(N, 128, T, 4)[rank, :, col].transpose(1, 0, 2)).reshape(128, 4 * T)
        for k in range(NB):
            W = mx_ref.quantize(np.ascontiguousarray(w[d][:, 512 * k:512 * k + 512]))
            y[d][:, BW * k:BW * k + BW] = mx_ref.matmul(W, mx_ref.quantize(np.ascontiguousarray(t[:, 4 * BW * k:4 * BW * k + 4 * BW])))
    return {"y": y, "ids": ids}

@@ -1,0 +1,330 @@
+from concourse.bass import DstId, RemoteDMATransfer
+from concourse.mybir import dt, AluOpType, ActivationFunctionType
+
+F32, BF, I32, U16 = "float32", "bfloat16", "int32", "uint16"
+CODE, PLANE = "float8_e4m3fn_x4", "uint8"
+SCRATCH = {
+    "ut": ("sbuf", [128, 512], BF),
+    "xt": ("sbuf", [128, 2048], BF), "wt": ("sbuf", [128, 2048], BF),
+    "uq": ("sbuf", [128, 128], CODE), "up": ("sbuf", [128, 128], PLANE),
+    "urq": ("sbuf", [128, 128], CODE), "urp": ("sbuf", [128, 128], PLANE),
+    "xq": ("sbuf", [128, 512], CODE), "xp": ("sbuf", [128, 512], PLANE),
+    "wq": ("sbuf", [128, 512], CODE), "wp": ("sbuf", [128, 512], PLANE),
+    "slotq": ("sbuf", [128, 512], CODE), "slotp": ("sbuf", [128, 512], PLANE),
+    "landq": ("sbuf", [128, 512], CODE), "landp": ("sbuf", [128, 512], PLANE),
+    "finq": ("sbuf", [128, 512], CODE), "finp": ("sbuf", [128, 512], PLANE),
+    "zoff": ("sbuf", [128, 8], U16), "colidx": ("sbuf", [128, 256], F32),
+    "mk0": ("sbuf", [128, 256], F32), "mk1": ("sbuf", [128, 256], F32),
+    "pi": ("sbuf", [128, 1], I32), "pa": ("sbuf", [128, 1], I32), "pb": ("sbuf", [128, 1], I32),
+    "pf": ("sbuf", [128, 1], F32), "paf": ("sbuf", [128, 1], F32), "pbf": ("sbuf", [128, 1], F32),
+    "tc0": ("sbuf", [128, 1], F32), "tc1": ("sbuf", [128, 1], F32), "g64": ("sbuf", [128, 1], F32),
+    "vfree": ("sbuf", [128, 64], F32), "vals": ("sbuf", [128, 64], BF),
+    "colf": ("sbuf", [32, 32], F32), "ocol": ("dram", [128, 4], F32), "rcol": ("dram", [8, 128, 4], F32),
+    "cr": ("sbuf", [128, 512], F32), "idb": ("sbuf", [128, 512], F32), "yb": ("sbuf", [128, 512], F32),
+}
+for _k in "ab":
+    for _n, _w, _d in (("sa", 64, F32), ("sb", 64, F32), ("dl", 4, F32), ("thr", 1024, F32), ("cmp", 2048, BF),
+                       ("rel", 512, BF), ("sgn", 512, BF), ("nlt", 8, F32), ("so", 1024, BF),
+                       ("pl", 4, U16), ("sw", 512, BF), ("tr", 512, BF), ("ya", 32, BF), ("yt", 32, BF),
+                       ("za", 32, BF), ("zb", 32, BF), ("uu", 64, BF), ("vt", 64, BF), ("off", 32, U16)):
+        SCRATCH[_n + _k] = ("sbuf", [128, _w], _d)
+for _k in range(8):
+    SCRATCH["ps%d" % _k] = ("psum", [128, 512], F32)
+
+SEMAPHORES = ["cv", "cs", "ct", "cg", "du", "dx0", "dx1", "dw", "dc", "dr", "dy", "di",
+              "ara", "arb", "arc", "ls"]
+
+PLAN = {"va": "m0 T0 m1 q1 t0 T1 i0 x2 i1 x0 x1 i2 z0 z1 i3 z2 z3", "sa": "d0 t1 d1 t2 r3 t3 s3",
+        "vb": "T0 T1 x1 t1 x2 x0 i0 i2 i1 z0 z2 i3 z1 z3", "sb": "d0 d1 t0 t2 r3 t3 s3"}
+
+
+def rank_program(g, core, T, topo):
+    me = T.rank_of(core)
+    if me is None:
+        return
+    V, S, P, Y = g.vector, g.scalar, g.tensor, g.sync
+    AF = ActivationFunctionType
+    Copy, Ident = AF.Copy, AF.Identity
+    GT, GE, LT = AluOpType.is_gt, AluOpType.is_ge, AluOpType.is_lt
+    ADD, MUL, AND = AluOpType.add, AluOpType.mult, AluOpType.bitwise_and
+    cnt, seen = {}, {}
+    queue = {"v": V, "s": S, "t": P, "g": g, "y": Y}
+    CORES = T.cores
+    N = len(CORES)
+    CH = 512 // N
+
+    def need(q, *toks):
+        for sem, val in toks:
+            if seen.get((q, sem), 0) < val:
+                queue[q].wait_ge(T.sem[sem], val)
+                seen[(q, sem)] = val
+
+    def done(q, inst):
+        sem = "c" + q
+        inst.then_inc(T.sem[sem], 1)
+        cnt[sem] = cnt.get(sem, 0) + 1
+        return (sem, cnt[sem])
+
+    def dma(sem, inst):
+        inst.then_inc(T.sem[sem], 16)
+        cnt[sem] = cnt.get(sem, 0) + 16
+        return (sem, cnt[sem])
+
+    tu = dma("du", S.dma_start(T.ut[:, 0:8], T.u[:, 0:8]))
+    tx = [dma("dx0", Y.dma_start(T.xt[:, 0:1024], T.x[:, 0:1024])),
+          dma("dx1", S.dma_start(T.xt[:, 1024:2048], T.x[:, 1024:2048]))]
+    need("y", *tx)
+    dma("dw", Y.dma_start(T.wt[:, 0:1024], T.w[:, 0:1024]))
+    tw = dma("dw", Y.dma_start(T.wt[:, 1024:2048], T.w[:, 1024:2048]))
+
+    tpi = done("g", g.iota(T.pi[:], [[1, 1]], 0, 1))
+    tpf = done("g", g.iota(T.pf[:], [[1, 1]], 0, 1, allow_small_or_imprecise_dtypes=True))
+    tci = done("g", g.iota(T.colidx[:], [[1, 256]], 0, 0, allow_small_or_imprecise_dtypes=True))
+    tvf = done("g", g.iota(T.vfree[:], [[256, 2], [32, 2], [1, 16]], -256, 0, allow_small_or_imprecise_dtypes=True))
+    tcr = done("g", g.iota(T.cr[:], [[1, N], [0, CH]], 0, 0, allow_small_or_imprecise_dtypes=True))
+
+    done("v", V.memset(T.ut[:, 8:512], 0.0))
+    tz = done("v", V.memset(T.zoff[:], 0))
+    need("v", tpi)
+    done("v", V.tensor_scalar(T.pa[:], T.pi[:], 96, None, AND))
+    t = done("v", V.tensor_scalar(T.pb[:], T.pi[:], 16, None, AND))
+    done("v", V.memset(T.swa[:], 0.0))
+    need("v", t)
+    done("v", V.tensor_copy(T.paf[:], T.pa[:]))
+    tpb = done("v", V.tensor_copy(T.pbf[:], T.pb[:]))
+
+    need("v", tu, tz)
+    tq = done("v", V.quantize_mx(T.uq[:], T.up[:], T.ut[:]))
+    need("v", tpf, tpb)
+    done("v", V.tensor_tensor(T.tc0[:], T.pf[:], T.paf[:], ADD))
+    tg64 = done("v", V.tensor_scalar(T.g64[:], T.paf[:], 2.0, T.pbf[:], MUL, ADD))
+    need("v", tq)
+    tur = done("v", V.tensor_copy(T.urq[:].bitcast(dt.uint32), T.uq[:].bitcast(dt.uint32).indirect(T.zoff[:])))
+    need("s", tq, tz)
+    tup = done("s", S.activation(T.urp[:], T.up[:].indirect(T.zoff[:]), Copy))
+    need("v", tg64)
+    ttc = done("v", V.tensor_scalar(T.tc1[:], T.tc0[:], 32.0, None, ADD))
+
+    MK = (T.mk0, T.mk1)
+    mkt = {}
+
+    def mask(i):
+        need("v", tci, ttc)
+        mkt[i] = done("v", V.tensor_scalar(MK[i][:], T.colidx[:], (T.tc0, T.tc1)[i][:], -1.0, LT, MUL))
+        if i == 1:
+            need("v", tvf)
+            done("v", V.tensor_scalar(T.vals[:], T.vfree[:], T.g64[:], None, ADD))
+            done("v", V.memset(T.yaa[:, 16:32], 0.0))
+        return mkt[i]
+
+    H = (slice(0, 64), slice(64, 128))
+    Q = [slice(32 * a, 32 * a + 32) for a in range(4)]
+
+    def row(ps, q, p, a, b, *toks):
+        need("t", tur, tup, *toks)
+        return done("t", P.matmul_mx(ps[:, 0:b - a], T.urq[:], T.urp[:], q[:, a:b], p[:, a:b], True, True))
+
+    def own(k, c):
+        return T[("sa", "sb")[c // 2] + k][:, 32 * (c % 2):32 * (c % 2) + 1]
+
+    def count(k, R, RS, tok, second=None):
+        cm, so, th, dl, rel, sgn, nlt = [T[n + k] for n in ("cmp", "so", "thr", "dl", "rel", "sgn", "nlt")]
+        vplan = PLAN["v" + k].split()
+        plan = {"v": list(vplan), "s": PLAN["s" + k].split()}
+        tok = dict(tok)
+        tok.update({"m%d" % i: mkt[i] for i in mkt})
+        front = ["i0", "i1"] + [x for x in vplan if x in ("x2", "x3")]
+
+        def deps(w):
+            c = int(w[1])
+            h = c // 2
+            return {"q": [], "m": [], "T": ["R%d" % c], "d": ["T%d" % c], "t": ["d%d" % h, "m%d" % (c % 2)], "i": ["t%d" % c],
+                    "x": ["T%d" % h, "R%d" % (1 - h)], "r": ["T%d" % h] + (front if RS is None else ["RS"]),
+                    "s": ["r%d" % c], "z": ["i%d" % c, ("x%d" if "x%d" % c in vplan else "s%d") % c]}[w[0]]
+
+        def emit(q, w):
+            c = int(w[1])
+            h, at, o = c // 2, 512 * c, 256 * (c % 2)
+            if w[0] == "q":
+                return second()
+            if w[0] == "m":
+                return mask(c)
+            need(q, *[tok[x] for x in deps(w)])
+            if w[0] == "T":
+                for a in range(4):
+                    tk = done("v", V.transpose(T[("sa", "sb")[c] + k][Q[a], 0:64], R[c][Q[a], 64 * a:64 * a + 64]))
+                return tk
+            if w[0] == "d":
+                return done("s", S.activation(dl[:, 2 * c:2 * c + 2], T[("sa", "sb")[c] + k][:, 0:64:32], AF.Abs,
+                                              bias=2.0 ** -120, scale=0.6 * 2.0 ** -23))
+            if w[0] == "t":
+                to = th[:, 256 * c:256 * c + 256]
+                if q == "s":
+                    return done("s", S.activation(to, MK[c % 2][:], Ident, bias=own(k, c), scale=dl[:, c:c + 1]))
+                return done("v", V.tensor_scalar(to, MK[c % 2][:], dl[:, c:c + 1], own(k, c), MUL, ADD))
+            if w[0] == "i":
+                return done("v", V.tensor_tensor(cm[:, at:at + 256], R[h][:, 0:256], th[:, 256 * c:256 * c + 256], GT))
+            if w[0] == "x":
+                return done("v", V.tensor_scalar(cm[:, at + 256:at + 512], R[1 - h][:, 0:256], own(k, c), None, (GT, GE)[h]))
+            if w[0] == "r":
+                src = R[0] if RS is None else RS
+                return done("s", S.activation(rel[:, o:o + 256], src[:, 0:256], AF.Relu, bias=own(k, c), scale=-1.0))
+            if w[0] == "s":
+                return done("s", S.activation(sgn[:, o:o + 256], rel[:, o:o + 256], AF.Sign, scale=-1.0,
+                                              accum_out=nlt[:, 4 * (c % 2):4 * (c % 2) + 1]))
+            if "x%d" % c in vplan:
+                return done("v", V.tensor_tensor_scan(so[:, 256 * c:256 * c + 256], cm[:, at:at + 256], cm[:, at + 256:at + 512],
+                                                      -256.0, ADD, ADD))
+            return done("v", V.tensor_tensor_scan(so[:, 256 * c + 128:256 * c + 256], cm[:, at:at + 128], cm[:, at + 128:at + 256],
+                                                  nlt[:, 4 * (c % 2):4 * (c % 2) + 1], ADD, ADD))
+
+        while plan["v"] or plan["s"]:
+            for q in "vs":
+                while plan[q] and all(x in tok for x in deps(plan[q][0])):
+                    w = plan[q].pop(0)
+                    tok["R1" if w == "q1" else w] = emit(q, w)
+        return tok[vplan[-1]]
+
+    def make_list(k, tok):
+        pl, sw, tr, ya, yt, za, zb, uu, vt, off = [T[n + k] for n in ("pl", "sw", "tr", "ya", "yt", "za", "zb", "uu", "vt", "off")]
+        need("v", tok)
+        tk = done("v", V.tensor_scalar(pl[:], T["so" + k][:, 255:1024:256], 256.0, None, ADD))
+        need("v", tk)
+        tk = done("v", V.tensor_copy(sw[:, 0:512].indirect(pl[:]), T.vals[:]))
+        need("v", tk)
+        tk = done("v", V.transpose(tr[:], sw[:]))
+        need("v", tk)
+        tk = done("v", V.tensor_tensor(ya[:, 0:16], tr[:, 0:512:32], tr[:, 16:512:32], ADD))
+        need("v", tk)
+        tk = done("v", V.transpose(yt[:], ya[:]))
+        need("v", tk)
+        done("v", V.tensor_tensor(za[H[0], :], yt[H[0], :], yt[H[1], :], ADD))
+        for a in range(2):
+            tk = done("v", V.tensor_tensor(zb[Q[a], :], yt[Q[a ^ 1], :], yt[Q[a ^ 3], :], ADD))
+        need("v", tk)
+        for j in (1, 2, 0, 3):
+            h = 16 * (j // 2)
+            tk = done("v", V.tensor_tensor(uu[H[0], 16 * j:16 * j + 16], za[H[0], h:h + 16], zb[H[0], h:h + 16], ADD))
+            if j == 2:
+                tf = tk
+        need("v", tk)
+        tk = done("v", V.transpose(vt[H[0], :], uu[H[0], :]))
+        need("v", tk)
+        for r in H:
+            done("v", V.tensor_scalar(off[r, 0:32:2], vt[H[0], 0:16], 256.0, None, ADD))
+            tk = done("v", V.tensor_scalar(off[r, 1:32:2], vt[H[0], 32:48], 256.0, None, ADD))
+        return tf, tk
+
+    RA, RB = T.ps0, T.ps1
+
+    def quant(h):
+        need("v", tx[h])
+        a, b = 256 * h, 256 * h + 256
+        return done("v", V.quantize_mx(T.xq[:, a:b], T.xp[:, a:b], T.xt[:, 4 * a:4 * b]))
+
+    tra = row(RA, T.xq, T.xp, 0, 256, quant(0))
+    tcount = count("a", (RA, RB), None, {"R0": tra}, lambda: row(RB, T.xq, T.xp, 256, 512, quant(1)))
+    tfo, tof = make_list("a", tcount)
+
+    need("s", tfo)
+    tcf = done("s", S.activation(T.colf[:], T.uua[Q[0], 16:48], Ident, bias=256.0))
+    need("v", tof)
+    need("s", tof)
+
+    def codes(dst, src, off, a, b):
+        return done("v", V.tensor_copy(dst[:, a:b].bitcast(dt.uint32), src[:].bitcast(dt.uint32).indirect(off[:, a // 16:b // 16])))
+
+    def scales(dst, src, off, a, b):
+        return done("s", S.activation(dst[:, a:b], src[:].indirect(off[:, a // 16:b // 16]), Copy))
+
+    def firsts(s):
+        return (N - 2, N - 1) if s < N // 2 else (0, 1)
+
+    lo, hi = (CH if me == 0 else 0), (512 - CH if me == N - 1 else 512)
+    fa, fb = CH * firsts(me)[0], CH * firsts(me)[1] + CH
+    rest = (lo, fa) if fa else (fb, hi)
+    tsc1 = scales(T.slotp, T.xp, T.offa, fa, fb)
+    tsc2 = scales(T.slotp, T.xp, T.offa, *rest)
+    codes(T.slotq, T.xq, T.offa, fa, fb)
+    tcode = codes(T.slotq, T.xq, T.offa, *rest)
+    ov = codes(T.landq, T.xq, T.offa, CH * me, CH * me + CH)
+    osc = scales(T.landp, T.xp, T.offa, CH * me, CH * me + CH)
+
+    others = [d for d in range(N) if d != me]
+    far = [d for d in others if topo.die(CORES[d]) != topo.die(core)]
+    near = [d for d in others if d not in far]
+    masks, wide = {}, {}
+    for grp, first in ((far, 0), (near, 1)):
+        for i, d in enumerate(grp):
+            el = topo.engines(core, CORES[d])
+            masks[d] = (1 << el[(4 * i + first) % len(el)]) | (1 << el[(4 * i + first + 2) % len(el)])
+    for i, d in enumerate(firsts(me)):
+        wide[d] = sum(1 << e for e in topo.engines(core, CORES[d])[i::2])
+    NW = len(topo.engines(core, CORES[firsts(me)[0]])) // 2
+    order = [others[(i + me) % len(others)] for i in range(len(others))]
+
+    def send(ds, eng, src, dst, sem):
+        tl = []
+        for d in ds:
+            rid, pid, _s = topo.addr(CORES[d])
+            tl.append(RemoteDMATransfer(dst_ids=[DstId(rid=rid, pnc=pid)], dma_engine_mask=eng[d],
+                                        remote_sem=T.sem[sem], src=src(d), dst=dst))
+        g.remote_dma_fused(tl, local_sem=T.sem.ls)
+        cnt["ls"] = cnt.get("ls", 0) + len(ds) * (NW if eng is wide else 2)
+
+    here = slice(CH * me, CH * me + CH)
+    half = "ara" if me < N // 2 else "arb"
+    need("g", tsc1)
+    send(firsts(me), wide, lambda d: T.slotp[:, CH * d:CH * d + CH], T.landp[:, here], half)
+    need("g", tcode)
+    send(order, masks, lambda d: T.slotq[:, CH * d:CH * d + CH].bitcast(dt.uint8), T.landq[:, here].bitcast(dt.uint8), half)
+    need("g", tsc2)
+    send([d for d in order if d not in firsts(me)], masks, lambda d: T.slotp[:, CH * d:CH * d + CH], T.landp[:, here], half)
+    need("y", tcf)
+    dma("dc", Y.dma_start(T.ocol[:], T.colf[0:16, :]))
+    tdc = dma("dc", Y.dma_start(T.rcol[me], T.colf[0:16, :]))
+    need("g", tdc)
+    send(order, masks, lambda d: T.ocol[:], T.rcol[me], "arc")
+    need("y", tdc, ("arc", 2 * (N - 1)), tcr)
+    tdr = dma("dr", Y.dma_start(T.cr[1:2, :], T.rcol[:, CH // 4 * me:CH // 4 * me + CH // 4, :]))
+
+    done("v", V.memset(T.swb[:], 0.0))
+    done("v", V.memset(T.yab[:, 16:32], 0.0))
+    need("v", tw)
+    twq = done("v", V.quantize_mx(T.wq[:], T.wp[:], T.wt[:]))
+
+    def landed(ranks):
+        return sum(2 + (NW if me in firsts(s) else 2) for s in ranks if s != me)
+
+    SA, SB, SC = T.ps3, T.ps4, T.ps5
+    tsa = row(SA, T.landq, T.landp, 0, 256, ("ara", landed(range(N // 2))), *((ov, osc) if me < N // 2 else ()))
+    tsb = row(SB, T.landq, T.landp, 256, 512, ("arb", landed(range(N // 2, N))), ov, osc)
+    tsc = row(SC, T.landq, T.landp, 0, 256)
+    _f, tof = make_list("b", count("b", (SA, SB), SC, {"R0": tsa, "R1": tsb, "RS": tsc}))
+
+    need("v", tof)
+    need("s", tof)
+    YP = (T.ps6, T.ps7, T.ps0, T.ps1)
+    ty = []
+    for k in range(4):
+        a, b = 128 * k, 128 * k + 128
+        if k % 2 == 0:
+            tv = codes(T.finq, T.landq, T.offb, a, a + 256)
+            ts = scales(T.finp, T.landp, T.offb, a, a + 256)
+        need("t", twq, tv, ts)
+        ty.append(done("t", P.matmul_mx(YP[k][:, 0:128], T.wq[:, a:b], T.wp[:, a:b], T.finq[:, a:b], T.finp[:, a:b], True, True)))
+    for k in (0, 2):
+        for b in (k, k + 1):
+            need("v", ty[b])
+            t = done("v", V.tensor_copy(T.yb[:, 128 * b:128 * b + 128], YP[b][:, 0:128]))
+        need("y", t)
+        dma("dy", Y.dma_start(T.y[:, 128 * k:128 * k + 256], T.yb[:, 128 * k:128 * k + 256]))
+    need("v", tdr)
+    ti1 = done("v", V.tensor_copy(T.idb[:, 0:128], T.cr[:].indirect(T.offb[:, 0:8])))
+    need("s", tdr)
+    ti2 = done("s", S.activation(T.idb[:, 128:512], T.cr[:].indirect(T.offb[:, 8:32]), Copy))
+    need("s", ti1, ti2)
+    dma("di", S.dma_start(T.ids[:], T.idb[0:2, :]))
+
+    for sem in ("cv", "cs", "ct", "cg", "dw", "dy", "di", "ls"):
+        need("g", (sem, cnt[sem]))

@@ -13,20 +13,19 @@ SCRATCH = {
     "slotq": ("sbuf", [128, 512], CODE), "slotp": ("sbuf", [128, 512], PLANE),
     "landq": ("sbuf", [128, 512], CODE), "landp": ("sbuf", [128, 512], PLANE),
     "finq": ("sbuf", [128, 512], CODE), "finp": ("sbuf", [128, 512], PLANE),
-    "zoff": ("sbuf", [128, 8], U16), "colidx": ("sbuf", [128, 256], F32),
-    "mk0": ("sbuf", [128, 256], F32), "mk1": ("sbuf", [128, 256], F32),
-    "pi": ("sbuf", [128, 1], I32), "pa": ("sbuf", [128, 1], I32), "pb": ("sbuf", [128, 1], I32),
-    "pf": ("sbuf", [128, 1], F32), "paf": ("sbuf", [128, 1], F32), "pbf": ("sbuf", [128, 1], F32),
-    "tc0": ("sbuf", [128, 1], F32), "tc1": ("sbuf", [128, 1], F32), "g64": ("sbuf", [128, 1], F32),
-    "vfree": ("sbuf", [128, 64], F32), "vals": ("sbuf", [128, 64], BF),
-    "colf": ("sbuf", [32, 32], F32), "ocol": ("dram", [128, 4], F32), "rcol": ("dram", [8, 128, 4], F32),
-    "cr": ("sbuf", [128, 512], F32), "idb": ("sbuf", [128, 512], F32), "yb": ("sbuf", [128, 512], F32),
+    "zoff": ("sbuf", [128, 8], U16), "colidx": ("sbuf", [128, 128], F32),
+    "mkr": ("sbuf", [128, 128], F32), "mk": ("sbuf", [128, 128], F32),
+    "lsrc": ("sbuf", [128, 128], F32), "ltr": ("sbuf", [128, 128], F32), "lc": ("sbuf", [128, 4], U16),
+    "inrun": ("sbuf", [128, 1], F32),
+    "dl": ("sbuf", [128, 4], F32), "thr": ("sbuf", [128, 512], F32),
+    "colt": ("sbuf", [32, 32], BF), "ocol": ("dram", [128, 4], BF), "rcol": ("dram", [8, 128, 4], BF),
+    "cr": ("sbuf", [128, 512], BF), "idb": ("sbuf", [128, 64], F32), "yb": ("sbuf", [128, 512], F32),
 }
 for _k in "ab":
-    for _n, _w, _d in (("sa", 64, F32), ("sb", 64, F32), ("dl", 4, F32), ("thr", 1024, F32), ("cmp", 2048, BF),
+    for _n, _w, _d in (("sa", 64, F32), ("sb", 64, F32), ("cmp", 2048, BF), ("vals", 64, BF),
                        ("rel", 512, BF), ("sgn", 512, BF), ("nlt", 8, F32), ("so", 1024, BF),
-                       ("pl", 4, U16), ("sw", 512, BF), ("tr", 512, BF), ("ya", 32, BF), ("yt", 32, BF),
-                       ("za", 32, BF), ("zb", 32, BF), ("uu", 64, BF), ("vt", 64, BF), ("off", 32, U16)):
+                       ("pl", 4, U16), ("sw", 544, BF), ("tr", 1056, BF), ("ya", 48, BF),
+                       ("za", 48, BF), ("zb", 48, BF), ("uu", 48, BF), ("off", 48, U16)):
         SCRATCH[_n + _k] = ("sbuf", [128, _w], _d)
 for _k in range(8):
     SCRATCH["ps%d" % _k] = ("psum", [128, 512], F32)
@@ -34,8 +33,8 @@ for _k in range(8):
 SEMAPHORES = ["cv", "cs", "ct", "cg", "du", "dx0", "dx1", "dw", "dc", "dr", "dy", "di",
               "ara", "arb", "arc", "ls"]
 
-PLAN = {"va": "m0 T0 m1 q1 t0 T1 i0 x2 i1 x0 x1 i2 z0 z1 i3 z2 z3", "sa": "d0 t1 d1 t2 r3 t3 s3",
-        "vb": "T0 T1 x1 t1 x2 x0 i0 i2 i1 z0 z2 i3 z1 z3", "sb": "d0 d1 t0 t2 r3 t3 s3"}
+PLAN = {"a": "vT0 sd0 vq1 st0 vn0 vn1 st1 vi0 vT1 vi1 sd1 vx0 sr3 vx1 st2 vn2 vn3 st3 vx2 vi2 ss3 vz0 vi3 vz1 vz2 vz3",
+        "b": "vT1 sr2 vA2 sr3 vA3 vx0 ss2 vB2 vB3 vx1 ss3 vA0 vA1 vz2 vB0 vB1 vz3 vz0 vz1"}
 
 
 def rank_program(g, core, T, topo):
@@ -45,13 +44,16 @@ def rank_program(g, core, T, topo):
     V, S, P, Y = g.vector, g.scalar, g.tensor, g.sync
     AF = ActivationFunctionType
     Copy, Ident = AF.Copy, AF.Identity
-    GT, GE, LT = AluOpType.is_gt, AluOpType.is_ge, AluOpType.is_lt
-    ADD, MUL, AND = AluOpType.add, AluOpType.mult, AluOpType.bitwise_and
+    GT, GE = AluOpType.is_gt, AluOpType.is_ge
+    ADD, MUL, MIN = AluOpType.add, AluOpType.mult, AluOpType.min
     cnt, seen = {}, {}
     queue = {"v": V, "s": S, "t": P, "g": g, "y": Y}
     CORES = T.cores
     N = len(CORES)
     CH = 512 // N
+    H = (slice(0, 64), slice(64, 128))
+    Q = [slice(32 * a, 32 * a + 32) for a in range(4)]
+    LAND = (0, 1, 2, 3, 4, 6, 5, 7)
 
     def need(q, *toks):
         for sem, val in toks:
@@ -70,6 +72,11 @@ def rank_program(g, core, T, topo):
         cnt[sem] = cnt.get(sem, 0) + 16
         return (sem, cnt[sem])
 
+    def iota(out, pattern, base, step, alone=False):
+        if alone:
+            need("g", ("cg", cnt["cg"]))
+        return done("g", g.iota(out, pattern, base, step, allow_small_or_imprecise_dtypes=True))
+
     tu = dma("du", S.dma_start(T.ut[:, 0:8], T.u[:, 0:8]))
     tx = [dma("dx0", Y.dma_start(T.xt[:, 0:1024], T.x[:, 0:1024])),
           dma("dx1", S.dma_start(T.xt[:, 1024:2048], T.x[:, 1024:2048]))]
@@ -77,143 +84,122 @@ def rank_program(g, core, T, topo):
     dma("dw", Y.dma_start(T.wt[:, 0:1024], T.w[:, 0:1024]))
     tw = dma("dw", Y.dma_start(T.wt[:, 1024:2048], T.w[:, 1024:2048]))
 
-    tpi = done("g", g.iota(T.pi[:], [[1, 1]], 0, 1))
-    tpf = done("g", g.iota(T.pf[:], [[1, 1]], 0, 1, allow_small_or_imprecise_dtypes=True))
-    tci = done("g", g.iota(T.colidx[:], [[1, 256]], 0, 0, allow_small_or_imprecise_dtypes=True))
-    tvf = done("g", g.iota(T.vfree[:], [[256, 2], [32, 2], [1, 16]], -256, 0, allow_small_or_imprecise_dtypes=True))
-    tcr = done("g", g.iota(T.cr[:], [[1, N], [0, CH]], 0, 0, allow_small_or_imprecise_dtypes=True))
+    for m in range(3):
+        iota(T.lsrc[:, 32 * m:32 * m + 16], [[8, 8], [136, 2]], 64 * (m % 2), m // 2)
+        iota(T.lsrc[:, 32 * m + 16:32 * m + 32], [[8, 8], [-128, 2]], 128 + (0, 64, 16)[m], m // 2)
+    tls = iota(T.lsrc[:, 96:128], [[128, 32]], 0, 1)
+    tci = iota(T.colidx[:], [[32, 128]], 0, 0)
+    iota(T.valsb[:, 0:32], [[128, 2], [1, 16]], -256, 1)
+    for a in range(4):
+        tva = iota(T.valsa[Q[a], :], [[128, 4], [4, 16]], a - 256, 4, True)
+    for a in range(4):
+        iota(T.valsb[Q[a], 32:64], [[64, 2], [2, 16]], 128 * (a // 2) + a % 2, 2, True)
+        iota(T.cmpb[Q[a], 1024:2048:512], [[0, 2]], a % 2, 2, True)
+    for r in H:
+        tvb = iota(T.inrun[r, :], [[1, 1]], -256, 1, True)
 
     done("v", V.memset(T.ut[:, 8:512], 0.0))
     tz = done("v", V.memset(T.zoff[:], 0))
-    need("v", tpi)
-    done("v", V.tensor_scalar(T.pa[:], T.pi[:], 96, None, AND))
-    t = done("v", V.tensor_scalar(T.pb[:], T.pi[:], 16, None, AND))
     done("v", V.memset(T.swa[:], 0.0))
-    need("v", t)
-    done("v", V.tensor_copy(T.paf[:], T.pa[:]))
-    tpb = done("v", V.tensor_copy(T.pbf[:], T.pb[:]))
 
     need("v", tu, tz)
     tq = done("v", V.quantize_mx(T.uq[:], T.up[:], T.ut[:]))
-    need("v", tpf, tpb)
-    done("v", V.tensor_tensor(T.tc0[:], T.pf[:], T.paf[:], ADD))
-    tg64 = done("v", V.tensor_scalar(T.g64[:], T.paf[:], 2.0, T.pbf[:], MUL, ADD))
     need("v", tq)
     tur = done("v", V.tensor_copy(T.urq[:].bitcast(dt.uint32), T.uq[:].bitcast(dt.uint32).indirect(T.zoff[:])))
     need("s", tq, tz)
     tup = done("s", S.activation(T.urp[:], T.up[:].indirect(T.zoff[:]), Copy))
-    need("v", tg64)
-    ttc = done("v", V.tensor_scalar(T.tc1[:], T.tc0[:], 32.0, None, ADD))
-
-    MK = (T.mk0, T.mk1)
-    mkt = {}
-
-    def mask(i):
-        need("v", tci, ttc)
-        mkt[i] = done("v", V.tensor_scalar(MK[i][:], T.colidx[:], (T.tc0, T.tc1)[i][:], -1.0, LT, MUL))
-        if i == 1:
-            need("v", tvf)
-            done("v", V.tensor_scalar(T.vals[:], T.vfree[:], T.g64[:], None, ADD))
-            done("v", V.memset(T.yaa[:, 16:32], 0.0))
-        return mkt[i]
-
-    H = (slice(0, 64), slice(64, 128))
-    Q = [slice(32 * a, 32 * a + 32) for a in range(4)]
 
     def row(ps, q, p, a, b, *toks):
         need("t", tur, tup, *toks)
         return done("t", P.matmul_mx(ps[:, 0:b - a], T.urq[:], T.urp[:], q[:, a:b], p[:, a:b], True, True))
 
-    def own(k, c):
-        return T[("sa", "sb")[c // 2] + k][:, 32 * (c % 2):32 * (c % 2) + 1]
-
-    def count(k, R, RS, tok, second=None):
-        cm, so, th, dl, rel, sgn, nlt = [T[n + k] for n in ("cmp", "so", "thr", "dl", "rel", "sgn", "nlt")]
-        vplan = PLAN["v" + k].split()
-        plan = {"v": list(vplan), "s": PLAN["s" + k].split()}
+    def count(k, R, own, tok, second=None):
+        cm, so, rel, sgn, nlt = [T[n + k] for n in ("cmp", "so", "rel", "sgn", "nlt")]
+        plan = PLAN[k].split()
         tok = dict(tok)
-        tok.update({"m%d" % i: mkt[i] for i in mkt})
-        front = ["i0", "i1"] + [x for x in vplan if x in ("x2", "x3")]
+        bank = {}
 
-        def deps(w):
-            c = int(w[1])
-            h = c // 2
-            return {"q": [], "m": [], "T": ["R%d" % c], "d": ["T%d" % c], "t": ["d%d" % h, "m%d" % (c % 2)], "i": ["t%d" % c],
-                    "x": ["T%d" % h, "R%d" % (1 - h)], "r": ["T%d" % h] + (front if RS is None else ["RS"]),
-                    "s": ["r%d" % c], "z": ["i%d" % c, ("x%d" if "x%d" % c in vplan else "s%d") % c]}[w[0]]
-
-        def emit(q, w):
-            c = int(w[1])
+        def emit(q, w, c):
             h, at, o = c // 2, 512 * c, 256 * (c % 2)
-            if w[0] == "q":
+            late = c % 2
+            if w == "q":
                 return second()
-            if w[0] == "m":
-                return mask(c)
-            need(q, *[tok[x] for x in deps(w)])
-            if w[0] == "T":
+            deps = {"T": ["R%d" % c], "d": ["T%d" % c], "t": ["d%d" % h], "i": ["t%d" % c], "n": ["T%d" % h],
+                    "A": ["O%d" % c, "R%d" % h], "B": ["A%d" % c], "x": ["O%d" % c, "R%d" % (1 - h)], "r": ["O%d" % c, "R0"],
+                    "s": ["r%d" % c], "z": [x + str(c) for x in "inBxs" if x + str(c) in tok]}[w]
+            b = {"T": c, "i": h, "n": h, "A": h, "B": h, "x": 1 - h, "r": 1 - h}.get(w)
+            need(q, *[tok[x] for x in deps])
+            need(q, *[t for (bb, qq), t in bank.items() if bb == b and qq != q])
+            if w == "T":
                 for a in range(4):
-                    tk = done("v", V.transpose(T[("sa", "sb")[c] + k][Q[a], 0:64], R[c][Q[a], 64 * a:64 * a + 64]))
-                return tk
-            if w[0] == "d":
-                return done("s", S.activation(dl[:, 2 * c:2 * c + 2], T[("sa", "sb")[c] + k][:, 0:64:32], AF.Abs,
-                                              bias=2.0 ** -120, scale=0.6 * 2.0 ** -23))
-            if w[0] == "t":
-                to = th[:, 256 * c:256 * c + 256]
+                    src = R[c][Q[a], a:256:4] if k == "a" else R[c][Q[a], 128 * (a // 2) + a % 2:128 * (a // 2) + 128:2]
+                    tk = done("v", V.transpose(T[("sa", "sb")[c] + k][Q[a], 0:64], src))
+                tok["O%d" % (2 * c)] = tok["O%d" % (2 * c + 1)] = tk
+            elif w == "d":
+                tk = done("s", S.activation(T.dl[:, 2 * c:2 * c + 2], T[("sa", "sb")[c] + k][:, 0:64:32], AF.Abs,
+                                            bias=2.0 ** -120, scale=0.6 * 2.0 ** -23))
+            elif w == "t":
+                need(q, tmk)
+                to = T.thr[:, 128 * c:128 * c + 128]
                 if q == "s":
-                    return done("s", S.activation(to, MK[c % 2][:], Ident, bias=own(k, c), scale=dl[:, c:c + 1]))
-                return done("v", V.tensor_scalar(to, MK[c % 2][:], dl[:, c:c + 1], own(k, c), MUL, ADD))
-            if w[0] == "i":
-                return done("v", V.tensor_tensor(cm[:, at:at + 256], R[h][:, 0:256], th[:, 256 * c:256 * c + 256], GT))
-            if w[0] == "x":
-                return done("v", V.tensor_scalar(cm[:, at + 256:at + 512], R[1 - h][:, 0:256], own(k, c), None, (GT, GE)[h]))
-            if w[0] == "r":
-                src = R[0] if RS is None else RS
-                return done("s", S.activation(rel[:, o:o + 256], src[:, 0:256], AF.Relu, bias=own(k, c), scale=-1.0))
-            if w[0] == "s":
-                return done("s", S.activation(sgn[:, o:o + 256], rel[:, o:o + 256], AF.Sign, scale=-1.0,
-                                              accum_out=nlt[:, 4 * (c % 2):4 * (c % 2) + 1]))
-            if "x%d" % c in vplan:
-                return done("v", V.tensor_tensor_scan(so[:, 256 * c:256 * c + 256], cm[:, at:at + 256], cm[:, at + 256:at + 512],
-                                                      -256.0, ADD, ADD))
-            return done("v", V.tensor_tensor_scan(so[:, 256 * c + 128:256 * c + 256], cm[:, at:at + 128], cm[:, at + 128:at + 256],
-                                                  nlt[:, 4 * (c % 2):4 * (c % 2) + 1], ADD, ADD))
+                    tk = done("s", S.activation(to, T.mk[:], Ident, bias=own(c), scale=T.dl[:, c:c + 1]))
+                else:
+                    tk = done("v", V.tensor_scalar(to, T.mk[:], T.dl[:, c:c + 1], own(c), MUL, ADD))
+            elif w == "i":
+                tk = done("v", V.tensor_tensor(cm[:, at:at + 128], R[h][:, 128 * late:128 * late + 128],
+                                               T.thr[:, 128 * c:128 * c + 128], GT))
+            elif w == "n":
+                tk = done("v", V.tensor_scalar(cm[:, at + 128:at + 256], R[h][:, 128 - 128 * late:256 - 128 * late], own(c), None,
+                                               (GT, GE)[late]))
+            elif w == "A":
+                tk = done("v", V.tensor_scalar(cm[:, at + h:at + h + 192], R[h][:, 64 - 64 * late:256 - 64 * late], own(c), None,
+                                               (GT, GE)[late]))
+            elif w == "B":
+                r, to = H[1 - late], at + h + (64 if h else 128 * late)
+                tk = done("v", V.tensor_scalar(cm[r, to:to + 64], R[h][r, 192 * late:192 * late + 64], own(c, r), None,
+                                               (GE, GT)[late]))
+            elif w == "x":
+                n = 256 if k == "a" else 192
+                tk = done("v", V.tensor_scalar(cm[:, at + n:at + n + 256], R[1 - h][:, 0:256], own(c), None, (GT, GE)[h]))
+            elif w == "r":
+                tk = done("s", S.activation(rel[:, o:o + 256], R[0][:, 0:256], AF.Relu, bias=own(c), scale=-1.0))
+            elif w == "s":
+                tk = done("s", S.activation(sgn[:, o:o + 256], rel[:, o:o + 256], AF.Sign, scale=-1.0,
+                                            accum_out=nlt[:, 4 * late:4 * late + 1]))
+            else:
+                across = "x%d" % c in tok
+                n = ((128, 256), (97, 224))[k == "b"][across]
+                first = (-256.0 if k == "a" else T.inrun[:]) if across else nlt[:, 4 * late:4 * late + 1]
+                tk = done("v", V.tensor_tensor_scan(so[:, 256 * c + 256 - n:256 * c + 256], cm[:, at:at + n], cm[:, at + n:at + 2 * n],
+                                                    first, ADD, ADD))
+            if b is not None:
+                bank[(b, q)] = tk
+            return tk
 
-        while plan["v"] or plan["s"]:
-            for q in "vs":
-                while plan[q] and all(x in tok for x in deps(plan[q][0])):
-                    w = plan[q].pop(0)
-                    tok["R1" if w == "q1" else w] = emit(q, w)
-        return tok[vplan[-1]]
+        for x in plan:
+            tok["R1" if x[1] == "q" else x[1:]] = tk = emit(x[0], x[1], int(x[2]))
+        return tk
 
-    def make_list(k, tok):
-        pl, sw, tr, ya, yt, za, zb, uu, vt, off = [T[n + k] for n in ("pl", "sw", "tr", "ya", "yt", "za", "zb", "uu", "vt", "off")]
-        need("v", tok)
+    def make_list(k, n, *tok):
+        pl, sw, tr, ya, za, zb, uu, off = [T[x + k] for x in ("pl", "sw", "tr", "ya", "za", "zb", "uu", "off")]
+        need("v", *tok)
         tk = done("v", V.tensor_scalar(pl[:], T["so" + k][:, 255:1024:256], 256.0, None, ADD))
         need("v", tk)
-        tk = done("v", V.tensor_copy(sw[:, 0:512].indirect(pl[:]), T.vals[:]))
+        tk = done("v", V.tensor_copy(sw[:, 16:528].indirect(pl[:]), T["vals" + k][:]))
         need("v", tk)
-        tk = done("v", V.transpose(tr[:], sw[:]))
+        done("v", V.transpose(tr[:, 0:512], sw[:, 16:528]))
+        tk = done("v", V.transpose(tr[:, 512:1056], sw[:]))
         need("v", tk)
-        tk = done("v", V.tensor_tensor(ya[:, 0:16], tr[:, 0:512:32], tr[:, 16:512:32], ADD))
+        tk = done("v", V.tensor_tensor(ya[:, 0:33], tr[:, 0:1056:32], tr[:, 16:1056:32], ADD))
         need("v", tk)
-        tk = done("v", V.transpose(yt[:], ya[:]))
-        need("v", tk)
-        done("v", V.tensor_tensor(za[H[0], :], yt[H[0], :], yt[H[1], :], ADD))
+        done("v", V.tensor_tensor(za[H[0], 0:33], ya[H[0], 0:33], ya[H[1], 0:33], ADD))
         for a in range(2):
-            tk = done("v", V.tensor_tensor(zb[Q[a], :], yt[Q[a ^ 1], :], yt[Q[a ^ 3], :], ADD))
-        need("v", tk)
-        for j in (1, 2, 0, 3):
-            h = 16 * (j // 2)
-            tk = done("v", V.tensor_tensor(uu[H[0], 16 * j:16 * j + 16], za[H[0], h:h + 16], zb[H[0], h:h + 16], ADD))
-            if j == 2:
-                tf = tk
-        need("v", tk)
-        tk = done("v", V.transpose(vt[H[0], :], uu[H[0], :]))
+            tk = done("v", V.tensor_tensor(zb[Q[a], 0:33], ya[Q[a ^ 1], 0:33], ya[Q[a ^ 3], 0:33], ADD))
         need("v", tk)
         for r in H:
-            done("v", V.tensor_scalar(off[r, 0:32:2], vt[H[0], 0:16], 256.0, None, ADD))
-            tk = done("v", V.tensor_scalar(off[r, 1:32:2], vt[H[0], 32:48], 256.0, None, ADD))
-        return tf, tk
+            tk = done("v", V.tensor_tensor(uu[r, 0:33], za[H[0], 0:33], zb[H[0], 0:33], ADD))
+        need("v", tk)
+        return done("v", V.tensor_scalar(off[:, 0:16 * n], uu[:, 0:33].indirect(T.lc[:, 0:n]), 256.0, None, ADD))
 
     RA, RB = T.ps0, T.ps1
 
@@ -222,33 +208,43 @@ def rank_program(g, core, T, topo):
         a, b = 256 * h, 256 * h + 256
         return done("v", V.quantize_mx(T.xq[:, a:b], T.xp[:, a:b], T.xt[:, 4 * a:4 * b]))
 
-    tra = row(RA, T.xq, T.xp, 0, 256, quant(0))
-    tcount = count("a", (RA, RB), None, {"R0": tra}, lambda: row(RB, T.xq, T.xp, 256, 512, quant(1)))
-    tfo, tof = make_list("a", tcount)
+    def owna(c):
+        return (T.saa, T.sba)[c // 2][:, 32 * (c % 2):32 * (c % 2) + 1]
 
-    need("s", tfo)
-    tcf = done("s", S.activation(T.colf[:], T.uua[Q[0], 16:48], Ident, bias=256.0))
+    tra = row(RA, T.xq, T.xp, 0, 256, quant(0))
+    need("v", tls)
+    t = done("v", V.transpose(T.ltr[:], T.lsrc[:]))
+    need("v", t)
+    done("v", V.tensor_scalar(T.lc[:, 0:3], T.ltr[:, 0:96:32], 0.125, 32.0, MUL, MIN))
+    need("s", t, tci)
+    t = done("s", S.activation(T.mkr[:], T.colidx[:], AF.Relu, bias=T.ltr[:, 96:97], scale=-1.0))
+    need("s", t)
+    tmk = done("s", S.activation(T.mk[:], T.mkr[:], AF.Sign, scale=-1.0))
+    tcount = count("a", (RA, RB), owna, {"R0": tra}, lambda: row(RB, T.xq, T.xp, 256, 512, quant(1)))
+    tof = make_list("a", 2, tcount, tva)
+
     need("v", tof)
     need("s", tof)
 
-    def codes(dst, src, off, a, b):
-        return done("v", V.tensor_copy(dst[:, a:b].bitcast(dt.uint32), src[:].bitcast(dt.uint32).indirect(off[:, a // 16:b // 16])))
+    def codes(dst, at, src, off, a, b):
+        return done("v", V.tensor_copy(dst[:, at:at + b - a].bitcast(dt.uint32), src[:].bitcast(dt.uint32).indirect(off[:, a // 16:b // 16])))
 
-    def scales(dst, src, off, a, b):
-        return done("s", S.activation(dst[:, a:b], src[:].indirect(off[:, a // 16:b // 16]), Copy))
+    def scales(dst, at, src, off, a, b):
+        return done("s", S.activation(dst[:, at:at + b - a], src[:].indirect(off[:, a // 16:b // 16]), Copy))
 
     def firsts(s):
         return (N - 2, N - 1) if s < N // 2 else (0, 1)
 
     lo, hi = (CH if me == 0 else 0), (512 - CH if me == N - 1 else 512)
     fa, fb = CH * firsts(me)[0], CH * firsts(me)[1] + CH
-    rest = (lo, fa) if fa else (fb, hi)
-    tsc1 = scales(T.slotp, T.xp, T.offa, fa, fb)
-    tsc2 = scales(T.slotp, T.xp, T.offa, *rest)
-    codes(T.slotq, T.xq, T.offa, fa, fb)
-    tcode = codes(T.slotq, T.xq, T.offa, *rest)
-    ov = codes(T.landq, T.xq, T.offa, CH * me, CH * me + CH)
-    osc = scales(T.landp, T.xp, T.offa, CH * me, CH * me + CH)
+    ra, rb = (lo, fa) if fa else (fb, hi)
+    tsc1 = scales(T.slotp, fa, T.xp, T.offa, fa, fb)
+    tsc2 = scales(T.slotp, ra, T.xp, T.offa, ra, rb)
+    codes(T.slotq, fa, T.xq, T.offa, fa, fb)
+    tcode = codes(T.slotq, ra, T.xq, T.offa, ra, rb)
+    ov = codes(T.landq, CH * LAND[me], T.xq, T.offa, CH * me, CH * me + CH)
+    osc = scales(T.landp, CH * LAND[me], T.xp, T.offa, CH * me, CH * me + CH)
+    tcf = done("v", V.transpose(T.colt[:], T.uua[Q[0], 0:32]))
 
     others = [d for d in range(N) if d != me]
     far = [d for d in others if topo.die(CORES[d]) != topo.die(core)]
@@ -272,7 +268,7 @@ def rank_program(g, core, T, topo):
         g.remote_dma_fused(tl, local_sem=T.sem.ls)
         cnt["ls"] = cnt.get("ls", 0) + len(ds) * (NW if eng is wide else 2)
 
-    here = slice(CH * me, CH * me + CH)
+    here = slice(CH * LAND[me], CH * LAND[me] + CH)
     half = "ara" if me < N // 2 else "arb"
     need("g", tsc1)
     send(firsts(me), wide, lambda d: T.slotp[:, CH * d:CH * d + CH], T.landp[:, here], half)
@@ -281,26 +277,35 @@ def rank_program(g, core, T, topo):
     need("g", tsc2)
     send([d for d in order if d not in firsts(me)], masks, lambda d: T.slotp[:, CH * d:CH * d + CH], T.landp[:, here], half)
     need("y", tcf)
-    dma("dc", Y.dma_start(T.ocol[:], T.colf[0:16, :]))
-    tdc = dma("dc", Y.dma_start(T.rcol[me], T.colf[0:16, :]))
+    dma("dc", Y.dma_start(T.ocol[:], T.colt[0:16, :]))
+    tdc = dma("dc", Y.dma_start(T.rcol[LAND[me]], T.colt[0:16, :]))
     need("g", tdc)
-    send(order, masks, lambda d: T.ocol[:], T.rcol[me], "arc")
+    send(order, masks, lambda d: T.ocol[:], T.rcol[LAND[me]], "arc")
+    iota(T.cr[:, 0:256], [[1, 4], [0, CH]], -256, 0, True)
+    tcr = iota(T.cr[:, 256:512], [[1, 2], [2, 2], [0, CH]], 4 - 256, 0)
     need("y", tdc, ("arc", 2 * (N - 1)), tcr)
-    tdr = dma("dr", Y.dma_start(T.cr[1:2, :], T.rcol[:, CH // 4 * me:CH // 4 * me + CH // 4, :]))
+    for r in range(8):
+        tdr = dma("dr", Y.dma_start(T.cr[16 * r + 1:16 * r + 2, :], T.rcol[:, CH // 4 * me:CH // 4 * me + CH // 4, :]))
 
     done("v", V.memset(T.swb[:], 0.0))
-    done("v", V.memset(T.yab[:, 16:32], 0.0))
-    need("v", tw)
+    done("v", V.memset(T.cmpb[:, 1024 + 193:2048:512], 0.0))
+    need("v", tw, tvb)
     twq = done("v", V.quantize_mx(T.wq[:], T.wp[:], T.wt[:]))
 
     def landed(ranks):
         return sum(2 + (NW if me in firsts(s) else 2) for s in ranks if s != me)
 
-    SA, SB, SC = T.ps3, T.ps4, T.ps5
-    tsa = row(SA, T.landq, T.landp, 0, 256, ("ara", landed(range(N // 2))), *((ov, osc) if me < N // 2 else ()))
-    tsb = row(SB, T.landq, T.landp, 256, 512, ("arb", landed(range(N // 2, N))), ov, osc)
-    tsc = row(SC, T.landq, T.landp, 0, 256)
-    _f, tof = make_list("b", count("b", (SA, SB), SC, {"R0": tsa, "R1": tsb, "RS": tsc}))
+    SA, SB, OWN = T.ps2, T.ps3, (T.ps4, T.ps5)
+
+    def ownb(c, r=slice(0, 128)):
+        return OWN[c][r, 0:1] if c < 2 else T.sbb[r, 32 * (c % 2):32 * (c % 2) + 1]
+
+    tok = {"R1": row(SB, T.landq, T.landp, 256, 512, ("arb", landed(range(N // 2, N))), ov, osc)}
+    tok["R0"] = row(SA, T.landq, T.landp, 0, 256, ("ara", landed(range(N // 2))))
+    for c in range(2):
+        a, b = 128 * c, 128 * c + 128
+        tok["O%d" % c] = done("t", P.matmul_mx(OWN[c][:, 0:128], T.landq[:, a:b], T.landp[:, a:b], T.uq[:], T.up[:], True, True))
+    tof = make_list("b", 3, count("b", (SA, SB), ownb, tok))
 
     need("v", tof)
     need("s", tof)
@@ -309,22 +314,24 @@ def rank_program(g, core, T, topo):
     for k in range(4):
         a, b = 128 * k, 128 * k + 128
         if k % 2 == 0:
-            tv = codes(T.finq, T.landq, T.offb, a, a + 256)
-            ts = scales(T.finp, T.landp, T.offb, a, a + 256)
+            tv = codes(T.finq, a, T.landq, T.offb, a, a + 256)
+            ts = scales(T.finp, a, T.landp, T.offb, a, a + 256)
         need("t", twq, tv, ts)
         ty.append(done("t", P.matmul_mx(YP[k][:, 0:128], T.wq[:, a:b], T.wp[:, a:b], T.finq[:, a:b], T.finp[:, a:b], True, True)))
-    for k in (0, 2):
-        for b in (k, k + 1):
-            need("v", ty[b])
-            t = done("v", V.tensor_copy(T.yb[:, 128 * b:128 * b + 128], YP[b][:, 0:128]))
-        need("y", t)
-        dma("dy", Y.dma_start(T.y[:, 128 * k:128 * k + 256], T.yb[:, 128 * k:128 * k + 256]))
-    need("v", tdr)
-    ti1 = done("v", V.tensor_copy(T.idb[:, 0:128], T.cr[:].indirect(T.offb[:, 0:8])))
     need("s", tdr)
-    ti2 = done("s", S.activation(T.idb[:, 128:512], T.cr[:].indirect(T.offb[:, 8:32]), Copy))
-    need("s", ti1, ti2)
-    dma("di", S.dma_start(T.ids[:], T.idb[0:2, :]))
+    ti = done("s", S.activation(T.idb[:], T.cr[:].indirect(T.offb[:, 32:36]), Ident, bias=256.0))
+    tc = []
+    for b, q in enumerate("vvvs"):
+        need(q, ty[b])
+        to, src = T.yb[:, 128 * b:128 * b + 128], YP[b][:, 0:128]
+        tc.append(done(q, V.tensor_copy(to, src) if q == "v" else S.activation(to, src, Copy)))
+    need("y", ti)
+    for r in range(2):
+        dma("di", Y.dma_start(T.ids[r:r + 1, :], T.idb[r:128:16, :]))
+    need("y", tc[1])
+    dma("dy", Y.dma_start(T.y[:, 0:256], T.yb[:, 0:256]))
+    need("s", tc[2], tc[3])
+    dma("dy", S.dma_start(T.y[:, 256:512], T.yb[:, 256:512]))
 
     for sem in ("cv", "cs", "ct", "cg", "dw", "dy", "di", "ls"):
         need("g", (sem, cnt[sem]))

@@ -14,12 +14,12 @@ SCRATCH = {
     "landq": ("sbuf", [128, 512], CODE), "landp": ("sbuf", [128, 512], PLANE),
     "finq": ("sbuf", [128, 512], CODE), "finp": ("sbuf", [128, 512], PLANE),
     "zoff": ("sbuf", [128, 8], U16), "colidx": ("sbuf", [128, 128], F32),
-    "mkr": ("sbuf", [128, 128], F32), "mk": ("sbuf", [128, 128], F32),
+    "mk": ("sbuf", [128, 128], F32),
     "lsrc": ("sbuf", [128, 128], F32), "ltr": ("sbuf", [128, 128], F32), "lc": ("sbuf", [128, 4], U16),
     "inrun": ("sbuf", [128, 1], F32),
     "dl": ("sbuf", [128, 4], F32), "thr": ("sbuf", [128, 512], F32),
-    "colt": ("sbuf", [32, 32], BF), "ocol": ("dram", [128, 4], BF), "rcol": ("dram", [8, 128, 4], BF),
-    "cr": ("sbuf", [128, 512], BF), "idb": ("sbuf", [128, 64], F32), "yb": ("sbuf", [128, 512], F32),
+    "colt": ("sbuf", [32, 32], BF), "rya": ("sbuf", [128, 16], BF), "rh": ("sbuf", [64, 16], BF), "rz": ("sbuf", [32, 32], BF),
+    "cr": ("sbuf", [128, 512], BF), "idb": ("sbuf", [128, 128], F32), "yb": ("sbuf", [128, 512], F32),
 }
 for _k in "ab":
     for _n, _w, _d in (("sa", 64, F32), ("sb", 64, F32), ("cmp", 2048, BF), ("vals", 64, BF),
@@ -30,7 +30,7 @@ for _k in "ab":
 for _k in range(8):
     SCRATCH["ps%d" % _k] = ("psum", [128, 512], F32)
 
-SEMAPHORES = ["cv", "cs", "ct", "cg", "du", "dx0", "dx1", "dw", "dc", "dr", "dy", "di",
+SEMAPHORES = ["cv", "cs", "ct", "cg", "du", "dx0", "dx1", "dw", "dr", "dy", "di",
               "ara", "arb", "arc", "ls"]
 
 PLAN = {"a": "vT0 sd0 vq1 st0 vn0 vn1 st1 vi0 vT1 vi1 sd1 vx0 sr3 vx1 st2 vn2 vn3 st3 vx2 vi2 ss3 vz0 vi3 vz1 vz2 vz3",
@@ -44,7 +44,7 @@ def rank_program(g, core, T, topo):
     V, S, P, Y = g.vector, g.scalar, g.tensor, g.sync
     AF = ActivationFunctionType
     Copy, Ident = AF.Copy, AF.Identity
-    GT, GE = AluOpType.is_gt, AluOpType.is_ge
+    GT, GE, LT = AluOpType.is_gt, AluOpType.is_ge, AluOpType.is_lt
     ADD, MUL, MIN = AluOpType.add, AluOpType.mult, AluOpType.min
     cnt, seen = {}, {}
     queue = {"v": V, "s": S, "t": P, "g": g, "y": Y}
@@ -79,28 +79,32 @@ def rank_program(g, core, T, topo):
 
     tu = dma("du", S.dma_start(T.ut[:, 0:8], T.u[:, 0:8]))
     tx = [dma("dx0", Y.dma_start(T.xt[:, 0:1024], T.x[:, 0:1024])),
-          dma("dx1", S.dma_start(T.xt[:, 1024:2048], T.x[:, 1024:2048]))]
+          dma("dx1", Y.dma_start(T.xt[:, 1024:2048], T.x[:, 1024:2048]))]
     need("y", *tx)
     dma("dw", Y.dma_start(T.wt[:, 0:1024], T.w[:, 0:1024]))
     tw = dma("dw", Y.dma_start(T.wt[:, 1024:2048], T.w[:, 1024:2048]))
 
-    for m in range(3):
-        iota(T.lsrc[:, 32 * m:32 * m + 16], [[8, 8], [136, 2]], 64 * (m % 2), m // 2)
-        iota(T.lsrc[:, 32 * m + 16:32 * m + 32], [[8, 8], [-128, 2]], 128 + (0, 64, 16)[m], m // 2)
-    tls = iota(T.lsrc[:, 96:128], [[128, 32]], 0, 1)
+    tps = iota(T.lsrc[:, 96:128], [[128, 32]], 0, 1)
     tci = iota(T.colidx[:], [[32, 128]], 0, 0)
+    for m in range(2):
+        iota(T.lsrc[:, 32 * m:32 * m + 16], [[8, 8], [136, 2]], 64 * m, 0)
+        tls = iota(T.lsrc[:, 32 * m + 16:32 * m + 32], [[8, 8], [-128, 2]], 128 + 64 * m, 0)
     iota(T.valsb[:, 0:32], [[128, 2], [1, 16]], -256, 1)
     for a in range(4):
         tva = iota(T.valsa[Q[a], :], [[128, 4], [4, 16]], a - 256, 4, True)
-    for a in range(4):
-        iota(T.valsb[Q[a], 32:64], [[64, 2], [2, 16]], 128 * (a // 2) + a % 2, 2, True)
-        iota(T.cmpb[Q[a], 1024:2048:512], [[0, 2]], a % 2, 2, True)
     for r in H:
-        tvb = iota(T.inrun[r, :], [[1, 1]], -256, 1, True)
+        iota(T.lsrc[r, 64:80], [[8, 8], [136, 2]], 0, 2, True)
+        iota(T.lsrc[r, 80:96], [[8, 8], [-128, 2]], 128 + 32, 2, True)
+    for a in range(4):
+        tvb = iota(T.valsb[Q[a], 32:64], [[64, 2], [2, 16]], 128 * (a // 2) + a % 2, 2, True)
+    iota(T.cr[:, 0:256], [[1, 4], [0, CH]], -256, 0, True)
+    tcr = iota(T.cr[:, 256:512], [[1, 2], [2, 2], [0, CH]], 4 - 256, 0)
 
     done("v", V.memset(T.ut[:, 8:512], 0.0))
     tz = done("v", V.memset(T.zoff[:], 0))
     done("v", V.memset(T.swa[:], 0.0))
+    need("v", tps)
+    done("v", V.transpose(T.ltr[:, 96:128], T.lsrc[:, 96:128]))
 
     need("v", tu, tz)
     tq = done("v", V.quantize_mx(T.uq[:], T.up[:], T.ut[:]))
@@ -123,10 +127,13 @@ def rank_program(g, core, T, topo):
             h, at, o = c // 2, 512 * c, 256 * (c % 2)
             late = c % 2
             if w == "q":
-                return second()
+                tk = second()
+                need(q, tok["T0"])
+                done("v", V.tensor_scalar(T.lc[:, 0:2], T.ltr[:, 0:64:32], 0.125, None, MUL))
+                return tk
             deps = {"T": ["R%d" % c], "d": ["T%d" % c], "t": ["d%d" % h], "i": ["t%d" % c], "n": ["T%d" % h],
                     "A": ["O%d" % c, "R%d" % h], "B": ["A%d" % c], "x": ["O%d" % c, "R%d" % (1 - h)], "r": ["O%d" % c, "R0"],
-                    "s": ["r%d" % c], "z": [x + str(c) for x in "inBxs" if x + str(c) in tok]}[w]
+                    "s": ["r%d" % c], "z": [x for x in tok if x == "run" or x[0] in "inBxs" and x[1:] == str(c)]}[w]
             b = {"T": c, "i": h, "n": h, "A": h, "B": h, "x": 1 - h, "r": 1 - h}.get(w)
             need(q, *[tok[x] for x in deps])
             need(q, *[t for (bb, qq), t in bank.items() if bb == b and qq != q])
@@ -190,8 +197,8 @@ def rank_program(g, core, T, topo):
         done("v", V.transpose(tr[:, 0:512], sw[:, 16:528]))
         tk = done("v", V.transpose(tr[:, 512:1056], sw[:]))
         need("v", tk)
-        tk = done("v", V.tensor_tensor(ya[:, 0:33], tr[:, 0:1056:32], tr[:, 16:1056:32], ADD))
-        need("v", tk)
+        t0 = done("v", V.tensor_tensor(ya[:, 0:33], tr[:, 0:1056:32], tr[:, 16:1056:32], ADD))
+        need("v", t0)
         done("v", V.tensor_tensor(za[H[0], 0:33], ya[H[0], 0:33], ya[H[1], 0:33], ADD))
         for a in range(2):
             tk = done("v", V.tensor_tensor(zb[Q[a], 0:33], ya[Q[a ^ 1], 0:33], ya[Q[a ^ 3], 0:33], ADD))
@@ -199,7 +206,7 @@ def rank_program(g, core, T, topo):
         for r in H:
             tk = done("v", V.tensor_tensor(uu[r, 0:33], za[H[0], 0:33], zb[H[0], 0:33], ADD))
         need("v", tk)
-        return done("v", V.tensor_scalar(off[:, 0:16 * n], uu[:, 0:33].indirect(T.lc[:, 0:n]), 256.0, None, ADD))
+        return t0, done("v", V.tensor_scalar(off[:, 0:16 * n], uu[:, 0:33].indirect(T.lc[:, 0:n]), 256.0, None, ADD))
 
     RA, RB = T.ps0, T.ps1
 
@@ -212,16 +219,12 @@ def rank_program(g, core, T, topo):
         return (T.saa, T.sba)[c // 2][:, 32 * (c % 2):32 * (c % 2) + 1]
 
     tra = row(RA, T.xq, T.xp, 0, 256, quant(0))
+    need("v", tci)
+    tmk = done("v", V.tensor_scalar(T.mk[:], T.colidx[:], T.ltr[:, 96:97], -1.0, LT, MUL))
     need("v", tls)
-    t = done("v", V.transpose(T.ltr[:], T.lsrc[:]))
-    need("v", t)
-    done("v", V.tensor_scalar(T.lc[:, 0:3], T.ltr[:, 0:96:32], 0.125, 32.0, MUL, MIN))
-    need("s", t, tci)
-    t = done("s", S.activation(T.mkr[:], T.colidx[:], AF.Relu, bias=T.ltr[:, 96:97], scale=-1.0))
-    need("s", t)
-    tmk = done("s", S.activation(T.mk[:], T.mkr[:], AF.Sign, scale=-1.0))
+    done("v", V.transpose(T.ltr[:, 0:64], T.lsrc[:, 0:64]))
     tcount = count("a", (RA, RB), owna, {"R0": tra}, lambda: row(RB, T.xq, T.xp, 256, 512, quant(1)))
-    tof = make_list("a", 2, tcount, tva)
+    tya, tof = make_list("a", 2, tcount, tva)
 
     need("v", tof)
     need("s", tof)
@@ -229,71 +232,75 @@ def rank_program(g, core, T, topo):
     def codes(dst, at, src, off, a, b):
         return done("v", V.tensor_copy(dst[:, at:at + b - a].bitcast(dt.uint32), src[:].bitcast(dt.uint32).indirect(off[:, a // 16:b // 16])))
 
-    def scales(dst, at, src, off, a, b):
-        return done("s", S.activation(dst[:, at:at + b - a], src[:].indirect(off[:, a // 16:b // 16]), Copy))
+    def scales(dst, at, src, off, a, b, q="s"):
+        to, win = dst[:, at:at + b - a], src[:].indirect(off[:, a // 16:b // 16])
+        return done(q, S.activation(to, win, Copy) if q == "s" else V.tensor_copy(to, win))
 
-    def firsts(s):
-        return (N - 2, N - 1) if s < N // 2 else (0, 1)
+    def lanes(s):
+        far = [d for d in range(N) if topo.die(CORES[d]) != topo.die(CORES[s])]
+        near = [d for d in range(N) if d != s and d not in far]
+        el = topo.engines(CORES[s], CORES[far[0]])
+        if near[1] != near[0] + 1:
+            near = near[1:] + near[:1]
+        ev, od = el[0::2], el[1::2]
+        pieces = {"A": far[:2], "B": far[2:], "C": near[:2], "D": near[2:]}
+        two = (ev[0:2], ev[2:4], ev[4:6], ev[6:8], od[0:2], od[2:4])
+        calls = [("p", {d: el[4 * i:4 * i + 4] for i, d in enumerate(far)}),
+                 ("q", dict(zip(far + near, two + (od[4:6],)))),
+                 ("p", dict(zip(near, (od[6:8], od[0:4], ev))))]
+        return pieces, calls, dict(zip(far + near, two + (od[4:8],)))
 
-    lo, hi = (CH if me == 0 else 0), (512 - CH if me == N - 1 else 512)
-    fa, fb = CH * firsts(me)[0], CH * firsts(me)[1] + CH
-    ra, rb = (lo, fa) if fa else (fb, hi)
-    tsc1 = scales(T.slotp, fa, T.xp, T.offa, fa, fb)
-    tsc2 = scales(T.slotp, ra, T.xp, T.offa, ra, rb)
-    codes(T.slotq, fa, T.xq, T.offa, fa, fb)
-    tcode = codes(T.slotq, ra, T.xq, T.offa, ra, rb)
+    pieces, calls, allq = lanes(me)
+    picked = {}
+    for q, kind, x in "spA vpB vqA spC vqB spD vqC vqD".split():
+        a, b = CH * pieces[x][0], CH * pieces[x][-1] + CH
+        tk = codes(T.slotq, a, T.xq, T.offa, a, b) if kind == "q" else scales(T.slotp, a, T.xp, T.offa, a, b, q)
+        picked.update({(kind, d): tk for d in pieces[x]})
     ov = codes(T.landq, CH * LAND[me], T.xq, T.offa, CH * me, CH * me + CH)
     osc = scales(T.landp, CH * LAND[me], T.xp, T.offa, CH * me, CH * me + CH)
-    tcf = done("v", V.transpose(T.colt[:], T.uua[Q[0], 0:32]))
 
-    others = [d for d in range(N) if d != me]
-    far = [d for d in others if topo.die(CORES[d]) != topo.die(core)]
-    near = [d for d in others if d not in far]
-    masks, wide = {}, {}
-    for grp, first in ((far, 0), (near, 1)):
-        for i, d in enumerate(grp):
-            el = topo.engines(core, CORES[d])
-            masks[d] = (1 << el[(4 * i + first) % len(el)]) | (1 << el[(4 * i + first + 2) % len(el)])
-    for i, d in enumerate(firsts(me)):
-        wide[d] = sum(1 << e for e in topo.engines(core, CORES[d])[i::2])
-    NW = len(topo.engines(core, CORES[firsts(me)[0]])) // 2
-    order = [others[(i + me) % len(others)] for i in range(len(others))]
-
-    def send(ds, eng, src, dst, sem):
+    def send(eng, src, dst, sem):
         tl = []
-        for d in ds:
+        for d in eng:
             rid, pid, _s = topo.addr(CORES[d])
-            tl.append(RemoteDMATransfer(dst_ids=[DstId(rid=rid, pnc=pid)], dma_engine_mask=eng[d],
+            tl.append(RemoteDMATransfer(dst_ids=[DstId(rid=rid, pnc=pid)], dma_engine_mask=sum(1 << e for e in eng[d]),
                                         remote_sem=T.sem[sem], src=src(d), dst=dst))
+            cnt["ls"] = cnt.get("ls", 0) + len(eng[d])
         g.remote_dma_fused(tl, local_sem=T.sem.ls)
-        cnt["ls"] = cnt.get("ls", 0) + len(ds) * (NW if eng is wide else 2)
 
     here = slice(CH * LAND[me], CH * LAND[me] + CH)
     half = "ara" if me < N // 2 else "arb"
-    need("g", tsc1)
-    send(firsts(me), wide, lambda d: T.slotp[:, CH * d:CH * d + CH], T.landp[:, here], half)
-    need("g", tcode)
-    send(order, masks, lambda d: T.slotq[:, CH * d:CH * d + CH].bitcast(dt.uint8), T.landq[:, here].bitcast(dt.uint8), half)
-    need("g", tsc2)
-    send([d for d in order if d not in firsts(me)], masks, lambda d: T.slotp[:, CH * d:CH * d + CH], T.landp[:, here], half)
-    need("y", tcf)
-    dma("dc", Y.dma_start(T.ocol[:], T.colt[0:16, :]))
-    tdc = dma("dc", Y.dma_start(T.rcol[LAND[me]], T.colt[0:16, :]))
-    need("g", tdc)
-    send(order, masks, lambda d: T.ocol[:], T.rcol[LAND[me]], "arc")
-    iota(T.cr[:, 0:256], [[1, 4], [0, CH]], -256, 0, True)
-    tcr = iota(T.cr[:, 256:512], [[1, 2], [2, 2], [0, CH]], 4 - 256, 0)
-    need("y", tdc, ("arc", 2 * (N - 1)), tcr)
-    for r in range(8):
-        tdr = dma("dr", Y.dma_start(T.cr[16 * r + 1:16 * r + 2, :], T.rcol[:, CH // 4 * me:CH // 4 * me + CH // 4, :]))
+    need("g", tya)
+    send(allq, lambda d: T.yaa[:, 2 * d:2 * d + 2], T.rya[:, 2 * LAND[me]:2 * LAND[me] + 2], "arc")
+    for kind, eng in calls:
+        need("g", *[picked[kind, d] for d in eng])
+        if kind == "p":
+            send(eng, lambda d: T.slotp[:, CH * d:CH * d + CH], T.landp[:, here], half)
+        else:
+            send(eng, lambda d: T.slotq[:, CH * d:CH * d + CH].bitcast(dt.uint8), T.landq[:, here].bitcast(dt.uint8), half)
+    for a in range(4):
+        iota(T.cmpb[Q[a], 1024:2048:512], [[0, 2]], a % 2, 2, True)
+    for r in H:
+        trun = iota(T.inrun[r, :], [[1, 1]], -256, 1, True)
 
-    done("v", V.memset(T.swb[:], 0.0))
-    done("v", V.memset(T.cmpb[:, 1024 + 193:2048:512], 0.0))
     need("v", tw, tvb)
     twq = done("v", V.quantize_mx(T.wq[:], T.wp[:], T.wt[:]))
+    t = done("v", V.transpose(T.ltr[:, 64:96], T.lsrc[:, 64:96]))
+    done("v", V.memset(T.rz[:, 16:32], 0.0))
+    need("v", t, ("arc", sum(len(lanes(s)[2].get(me, ())) for s in range(N))))
+    t = done("v", V.tensor_copy(T.rya[:, 2 * LAND[me]:2 * LAND[me] + 2], T.yaa[:, 2 * me:2 * me + 2]))
+    done("v", V.memset(T.cmpb[:, 1024 + 193:2048:512], 0.0))
+    done("v", V.tensor_scalar(T.lc[:, 2:3], T.ltr[:, 64:65], 0.125, 32.0, MUL, MIN))
+    need("v", t)
+    need("v", done("v", V.tensor_tensor(T.rh[:], T.rya[H[0], :], T.rya[H[1], :], ADD)))
+    need("v", done("v", V.tensor_tensor(T.rz[:, 0:16], T.rh[Q[0], :], T.rh[Q[1], :], ADD)))
+    need("y", done("v", V.transpose(T.colt[:], T.rz[:])), tcr)
+    done("v", V.memset(T.swb[:], 0.0))
+    for r in range(64, 128, 16):
+        tdr = dma("dr", Y.dma_start(T.cr[r:r + 1, :], T.colt[0:16, :]))
 
     def landed(ranks):
-        return sum(2 + (NW if me in firsts(s) else 2) for s in ranks if s != me)
+        return sum(len(eng.get(me, ())) for s in ranks for _k, eng in lanes(s)[1])
 
     SA, SB, OWN = T.ps2, T.ps3, (T.ps4, T.ps5)
 
@@ -301,11 +308,12 @@ def rank_program(g, core, T, topo):
         return OWN[c][r, 0:1] if c < 2 else T.sbb[r, 32 * (c % 2):32 * (c % 2) + 1]
 
     tok = {"R1": row(SB, T.landq, T.landp, 256, 512, ("arb", landed(range(N // 2, N))), ov, osc)}
+    tok["run"] = trun
     tok["R0"] = row(SA, T.landq, T.landp, 0, 256, ("ara", landed(range(N // 2))))
     for c in range(2):
         a, b = 128 * c, 128 * c + 128
         tok["O%d" % c] = done("t", P.matmul_mx(OWN[c][:, 0:128], T.landq[:, a:b], T.landp[:, a:b], T.uq[:], T.up[:], True, True))
-    tof = make_list("b", 3, count("b", (SA, SB), ownb, tok))
+    _t, tof = make_list("b", 3, count("b", (SA, SB), ownb, tok))
 
     need("v", tof)
     need("s", tof)
@@ -319,19 +327,17 @@ def rank_program(g, core, T, topo):
         need("t", twq, tv, ts)
         ty.append(done("t", P.matmul_mx(YP[k][:, 0:128], T.wq[:, a:b], T.wp[:, a:b], T.finq[:, a:b], T.finp[:, a:b], True, True)))
     need("s", tdr)
-    ti = done("s", S.activation(T.idb[:], T.cr[:].indirect(T.offb[:, 32:36]), Ident, bias=256.0))
+    ti = done("s", S.activation(T.idb[:], T.cr[:].indirect(T.offb[:, 32:40]), Ident, bias=256.0))
     tc = []
-    for b, q in enumerate("vvvs"):
+    for b, q in enumerate("vvsv"):
         need(q, ty[b])
         to, src = T.yb[:, 128 * b:128 * b + 128], YP[b][:, 0:128]
         tc.append(done(q, V.tensor_copy(to, src) if q == "v" else S.activation(to, src, Copy)))
     need("y", ti)
-    for r in range(2):
-        dma("di", Y.dma_start(T.ids[r:r + 1, :], T.idb[r:128:16, :]))
-    need("y", tc[1])
-    dma("dy", Y.dma_start(T.y[:, 0:256], T.yb[:, 0:256]))
-    need("s", tc[2], tc[3])
-    dma("dy", S.dma_start(T.y[:, 256:512], T.yb[:, 256:512]))
+    dma("di", Y.dma_start(T.ids[:], T.idb[0:128:16, :]))
+    for q, a in (("y", 0), ("s", 2)):
+        need(q, *tc[a:a + 2])
+        dma("dy", queue[q].dma_start(T.y[:, 128 * a:128 * a + 256], T.yb[:, 128 * a:128 * a + 256]))
 
-    for sem in ("cv", "cs", "ct", "cg", "dw", "dy", "di", "ls"):
+    for sem in ("cg", "ls", "dw", "ct", "cv", "cs", "di", "dy"):
         need("g", (sem, cnt[sem]))

@@ -18,7 +18,8 @@ SCRATCH = {
     "lsrc": ("sbuf", [128, 128], F32), "ltr": ("sbuf", [128, 128], F32), "lc": ("sbuf", [128, 4], U16),
     "inrun": ("sbuf", [128, 1], F32),
     "dl": ("sbuf", [128, 4], F32), "thr": ("sbuf", [128, 512], F32),
-    "colt": ("sbuf", [32, 32], BF), "rya": ("sbuf", [128, 16], BF), "rh": ("sbuf", [64, 16], BF), "rz": ("sbuf", [32, 32], BF),
+    "colt": ("sbuf", [32, 32], BF), "yc": ("sbuf", [128, 32], BF), "rya": ("sbuf", [128, 32], BF), "rg": ("sbuf", [128, 16], BF),
+    "rh": ("sbuf", [64, 16], BF), "rz": ("sbuf", [32, 32], BF),
     "cr": ("sbuf", [128, 512], BF), "idb": ("sbuf", [128, 128], F32), "yb": ("sbuf", [128, 512], F32),
 }
 for _k in "ab":
@@ -30,11 +31,11 @@ for _k in "ab":
 for _k in range(8):
     SCRATCH["ps%d" % _k] = ("psum", [128, 512], F32)
 
-SEMAPHORES = ["cv", "cs", "ct", "cg", "du", "dx0", "dx1", "dw", "dr", "dy", "di",
+SEMAPHORES = ["cv", "cs", "ct", "cg", "du", "dx0", "dx1", "dx2", "dw", "dr", "dy", "di",
               "ara", "arb", "arc", "ls"]
 
 PLAN = {"a": "vT0 sd0 vq1 st0 vn0 vn1 st1 vi0 vT1 vi1 sd1 vx0 sr3 vx1 st2 vn2 vn3 st3 vx2 vi2 ss3 vz0 vi3 vz1 vz2 vz3",
-        "b": "vT1 sr2 vA2 sr3 vA3 vx0 ss2 vB2 vB3 vx1 ss3 vA0 vA1 vz2 vB0 vB1 vz3 vz0 vz1"}
+        "b": "vT1 vA2 vA3 sr2 sr3 vB2 vB3 vx0 vx1 ss2 ss3 vA0 vA1 vz2 vB0 vB1 vz3 vz0 vz1"}
 
 
 def rank_program(g, core, T, topo):
@@ -53,7 +54,16 @@ def rank_program(g, core, T, topo):
     CH = 512 // N
     H = (slice(0, 64), slice(64, 128))
     Q = [slice(32 * a, 32 * a + 32) for a in range(4)]
-    LAND = (0, 1, 2, 3, 4, 6, 5, 7)
+
+    def sides(s):
+        home = [d for d in range(N) if topo.die(CORES[d]) == topo.die(CORES[s])]
+        return home, [d for d in range(N) if d not in home]
+
+    def land(s, d):
+        home, far = sides(d)
+        return home.index(s) if s in home else (4, 6, 5, 7)[far.index(s)]
+
+    flip = sides(me)[1][0] < me
 
     def need(q, *toks):
         for sem, val in toks:
@@ -77,9 +87,10 @@ def rank_program(g, core, T, topo):
             need("g", ("cg", cnt["cg"]))
         return done("g", g.iota(out, pattern, base, step, allow_small_or_imprecise_dtypes=True))
 
-    tu = dma("du", S.dma_start(T.ut[:, 0:8], T.u[:, 0:8]))
-    tx = [dma("dx0", Y.dma_start(T.xt[:, 0:1024], T.x[:, 0:1024])),
-          dma("dx1", Y.dma_start(T.xt[:, 1024:2048], T.x[:, 1024:2048]))]
+    tu = dma("du", Y.dma_start(T.ut[:, 0:8], T.u[:, 0:8]))
+    tx = [dma("dx0", S.dma_start(T.xt[:, 0:512], T.x[:, 0:512])),
+          dma("dx1", Y.dma_start(T.xt[:, 512:1024], T.x[:, 512:1024])),
+          dma("dx2", S.dma_start(T.xt[:, 1024:2048], T.x[:, 1024:2048]))]
     need("y", *tx)
     dma("dw", Y.dma_start(T.wt[:, 0:1024], T.w[:, 0:1024]))
     tw = dma("dw", Y.dma_start(T.wt[:, 1024:2048], T.w[:, 1024:2048]))
@@ -97,17 +108,15 @@ def rank_program(g, core, T, topo):
         iota(T.lsrc[r, 80:96], [[8, 8], [-128, 2]], 128 + 32, 2, True)
     for a in range(4):
         tvb = iota(T.valsb[Q[a], 32:64], [[64, 2], [2, 16]], 128 * (a // 2) + a % 2, 2, True)
-    iota(T.cr[:, 0:256], [[1, 4], [0, CH]], -256, 0, True)
-    tcr = iota(T.cr[:, 256:512], [[1, 2], [2, 2], [0, CH]], 4 - 256, 0)
 
     done("v", V.memset(T.ut[:, 8:512], 0.0))
     tz = done("v", V.memset(T.zoff[:], 0))
     done("v", V.memset(T.swa[:], 0.0))
-    need("v", tps)
-    done("v", V.transpose(T.ltr[:, 96:128], T.lsrc[:, 96:128]))
 
     need("v", tu, tz)
     tq = done("v", V.quantize_mx(T.uq[:], T.up[:], T.ut[:]))
+    need("v", tps)
+    tps = done("v", V.transpose(T.ltr[:, 96:128], T.lsrc[:, 96:128]))
     need("v", tq)
     tur = done("v", V.tensor_copy(T.urq[:].bitcast(dt.uint32), T.uq[:].bitcast(dt.uint32).indirect(T.zoff[:])))
     need("s", tq, tz)
@@ -121,6 +130,7 @@ def rank_program(g, core, T, topo):
         cm, so, rel, sgn, nlt = [T[n + k] for n in ("cmp", "so", "rel", "sgn", "nlt")]
         plan = PLAN[k].split()
         tok = dict(tok)
+        turn = int(k == "b" and flip)
         bank = {}
 
         def emit(q, w, c):
@@ -133,7 +143,7 @@ def rank_program(g, core, T, topo):
                 return tk
             deps = {"T": ["R%d" % c], "d": ["T%d" % c], "t": ["d%d" % h], "i": ["t%d" % c], "n": ["T%d" % h],
                     "A": ["O%d" % c, "R%d" % h], "B": ["A%d" % c], "x": ["O%d" % c, "R%d" % (1 - h)], "r": ["O%d" % c, "R0"],
-                    "s": ["r%d" % c], "z": [x for x in tok if x == "run" or x[0] in "inBxs" and x[1:] == str(c)]}[w]
+                    "s": ["r%d" % c], "z": [x for x in tok if x in ("run", "zero") or x[0] in "inBxs" and x[1:] == str(c)]}[w]
             b = {"T": c, "i": h, "n": h, "A": h, "B": h, "x": 1 - h, "r": 1 - h}.get(w)
             need(q, *[tok[x] for x in deps])
             need(q, *[t for (bb, qq), t in bank.items() if bb == b and qq != q])
@@ -167,11 +177,11 @@ def rank_program(g, core, T, topo):
                                                (GE, GT)[late]))
             elif w == "x":
                 n = 256 if k == "a" else 192
-                tk = done("v", V.tensor_scalar(cm[:, at + n:at + n + 256], R[1 - h][:, 0:256], own(c), None, (GT, GE)[h]))
+                tk = done("v", V.tensor_scalar(cm[:, at + n:at + n + 256], R[1 - h][:, 0:256], own(c), None, (GT, GE)[h ^ turn]))
             elif w == "r":
-                tk = done("s", S.activation(rel[:, o:o + 256], R[0][:, 0:256], AF.Relu, bias=own(c), scale=-1.0))
+                tk = done("s", S.activation(rel[:, o:o + 256], R[0][:, 0:256], (AF.Relu, AF.Sign)[turn], bias=own(c), scale=-1.0))
             elif w == "s":
-                tk = done("s", S.activation(sgn[:, o:o + 256], rel[:, o:o + 256], AF.Sign, scale=-1.0,
+                tk = done("s", S.activation(sgn[:, o:o + 256], rel[:, o:o + 256], (AF.Sign, AF.Relu)[turn], scale=-1.0,
                                             accum_out=nlt[:, 4 * late:4 * late + 1]))
             else:
                 across = "x%d" % c in tok
@@ -194,11 +204,11 @@ def rank_program(g, core, T, topo):
         need("v", tk)
         tk = done("v", V.tensor_copy(sw[:, 16:528].indirect(pl[:]), T["vals" + k][:]))
         need("v", tk)
-        done("v", V.transpose(tr[:, 0:512], sw[:, 16:528]))
+        t0 = done("v", V.transpose(tr[:, 0:512], sw[:, 16:528]))
         tk = done("v", V.transpose(tr[:, 512:1056], sw[:]))
         need("v", tk)
-        t0 = done("v", V.tensor_tensor(ya[:, 0:33], tr[:, 0:1056:32], tr[:, 16:1056:32], ADD))
-        need("v", t0)
+        tk = done("v", V.tensor_tensor(ya[:, 0:33], tr[:, 0:1056:32], tr[:, 16:1056:32], ADD))
+        need("v", tk)
         done("v", V.tensor_tensor(za[H[0], 0:33], ya[H[0], 0:33], ya[H[1], 0:33], ADD))
         for a in range(2):
             tk = done("v", V.tensor_tensor(zb[Q[a], 0:33], ya[Q[a ^ 1], 0:33], ya[Q[a ^ 3], 0:33], ADD))
@@ -210,21 +220,24 @@ def rank_program(g, core, T, topo):
 
     RA, RB = T.ps0, T.ps1
 
-    def quant(h):
-        need("v", tx[h])
-        a, b = 256 * h, 256 * h + 256
+    def quant(i):
+        need("v", tx[i])
+        a, b = (0, 128, 256, 512)[i:i + 2]
         return done("v", V.quantize_mx(T.xq[:, a:b], T.xp[:, a:b], T.xt[:, 4 * a:4 * b]))
 
     def owna(c):
         return (T.saa, T.sba)[c // 2][:, 32 * (c % 2):32 * (c % 2) + 1]
 
-    tra = row(RA, T.xq, T.xp, 0, 256, quant(0))
-    need("v", tci)
+    quant(0)
+    tra = row(RA, T.xq, T.xp, 0, 256, quant(1))
+    need("v", tci, tps)
     tmk = done("v", V.tensor_scalar(T.mk[:], T.colidx[:], T.ltr[:, 96:97], -1.0, LT, MUL))
     need("v", tls)
     done("v", V.transpose(T.ltr[:, 0:64], T.lsrc[:, 0:64]))
-    tcount = count("a", (RA, RB), owna, {"R0": tra}, lambda: row(RB, T.xq, T.xp, 256, 512, quant(1)))
-    tya, tof = make_list("a", 2, tcount, tva)
+    tcount = count("a", (RA, RB), owna, {"R0": tra}, lambda: row(RB, T.xq, T.xp, 256, 512, quant(2)))
+    t, tof = make_list("a", 2, tcount, tva)
+    need("s", t)
+    tya = done("s", S.activation(T.yc[:], T.tra[:, 0:512:16], Copy))
 
     need("v", tof)
     need("s", tof)
@@ -237,79 +250,78 @@ def rank_program(g, core, T, topo):
         return done(q, S.activation(to, win, Copy) if q == "s" else V.tensor_copy(to, win))
 
     def lanes(s):
-        far = [d for d in range(N) if topo.die(CORES[d]) != topo.die(CORES[s])]
-        near = [d for d in range(N) if d != s and d not in far]
+        home, far = sides(s)
+        near = [d for d in home if d != s]
         el = topo.engines(CORES[s], CORES[far[0]])
-        if near[1] != near[0] + 1:
-            near = near[1:] + near[:1]
         ev, od = el[0::2], el[1::2]
-        pieces = {"A": far[:2], "B": far[2:], "C": near[:2], "D": near[2:]}
-        two = (ev[0:2], ev[2:4], ev[4:6], ev[6:8], od[0:2], od[2:4])
-        calls = [("p", {d: el[4 * i:4 * i + 4] for i, d in enumerate(far)}),
-                 ("q", dict(zip(far + near, two + (od[4:6],)))),
-                 ("p", dict(zip(near, (od[6:8], od[0:4], ev))))]
-        return pieces, calls, dict(zip(far + near, two + (od[4:8],)))
+        four = {d: el[4 * i:4 * i + 4] for i, d in enumerate(far)}
+        calls = [("q", four), ("p", four), ("q", dict(zip(near, (od[:4], od[4:], ev)))),
+                 ("p", dict(zip(near, (ev[:4], ev[4:], od))))]
+        return calls, dict(zip(far + near, (ev[0:2], ev[2:4], ev[4:6], ev[6:8], od[0:2], od[2:4], od[4:8])))
 
-    pieces, calls, allq = lanes(me)
-    picked = {}
-    for q, kind, x in "spA vpB vqA spC vqB spD vqC vqD".split():
-        a, b = CH * pieces[x][0], CH * pieces[x][-1] + CH
-        tk = codes(T.slotq, a, T.xq, T.offa, a, b) if kind == "q" else scales(T.slotp, a, T.xp, T.offa, a, b, q)
-        picked.update({(kind, d): tk for d in pieces[x]})
-    ov = codes(T.landq, CH * LAND[me], T.xq, T.offa, CH * me, CH * me + CH)
-    osc = scales(T.landp, CH * LAND[me], T.xp, T.offa, CH * me, CH * me + CH)
+    calls, allq = lanes(me)
+    picked = []
+    for kind, eng in calls:
+        a, b = CH * min(eng), CH * max(eng) + CH
+        picked.append((codes(T.slotq, a, T.xq, T.offa, a, b) if kind == "q" else scales(T.slotp, a, T.xp, T.offa, a, b)))
+    ov = codes(T.landq, CH * land(me, me), T.xq, T.offa, CH * me, CH * me + CH)
+    osc = scales(T.landp, CH * land(me, me), T.xp, T.offa, CH * me, CH * me + CH)
 
-    def send(eng, src, dst, sem):
+    def send(eng, src, dst, w, sem=None):
         tl = []
         for d in eng:
             rid, pid, _s = topo.addr(CORES[d])
+            a, b = src[:, w * d:w * d + w], dst[:, w * land(me, d):w * land(me, d) + w]
+            if src.name == "slotq":
+                a, b = a.bitcast(dt.uint8), b.bitcast(dt.uint8)
             tl.append(RemoteDMATransfer(dst_ids=[DstId(rid=rid, pnc=pid)], dma_engine_mask=sum(1 << e for e in eng[d]),
-                                        remote_sem=T.sem[sem], src=src(d), dst=dst))
+                                        remote_sem=T.sem[sem or ("ara" if d in sides(me)[0] else "arb")], src=a, dst=b))
             cnt["ls"] = cnt.get("ls", 0) + len(eng[d])
         g.remote_dma_fused(tl, local_sem=T.sem.ls)
 
-    here = slice(CH * LAND[me], CH * LAND[me] + CH)
-    half = "ara" if me < N // 2 else "arb"
     need("g", tya)
-    send(allq, lambda d: T.yaa[:, 2 * d:2 * d + 2], T.rya[:, 2 * LAND[me]:2 * LAND[me] + 2], "arc")
-    for kind, eng in calls:
-        need("g", *[picked[kind, d] for d in eng])
-        if kind == "p":
-            send(eng, lambda d: T.slotp[:, CH * d:CH * d + CH], T.landp[:, here], half)
-        else:
-            send(eng, lambda d: T.slotq[:, CH * d:CH * d + CH].bitcast(dt.uint8), T.landq[:, here].bitcast(dt.uint8), half)
+    send(allq, T.yc, T.rya, 4, "arc")
+    for (kind, eng), tk in zip(calls, picked):
+        need("g", tk)
+        send(eng, T["slot" + kind], T["land" + kind], CH)
     for a in range(4):
-        iota(T.cmpb[Q[a], 1024:2048:512], [[0, 2]], a % 2, 2, True)
+        iota(T.cmpb[Q[a], 1024:2048:512], [[0, 2]], a % 2 - 256 * flip, 2, True)
     for r in H:
         trun = iota(T.inrun[r, :], [[1, 1]], -256, 1, True)
+    iota(T.cr[:, 0:256], [[1, 4], [0, CH]], sides(me)[0][0] - 256, 0, True)
+    tcr = iota(T.cr[:, 256:512], [[1, 2], [2, 2], [0, CH]], sides(me)[1][0] - 256, 0)
 
     need("v", tw, tvb)
     twq = done("v", V.quantize_mx(T.wq[:], T.wp[:], T.wt[:]))
+    need("s", tya, ("arc", sum(len(lanes(s)[1].get(me, ())) for s in range(N))))
+    done("s", S.activation(T.rz[:, 16:32], T.ut[Q[0], 8:24], Copy))
+    town = done("s", S.activation(T.rya[:, 4 * land(me, me):4 * land(me, me) + 4], T.yc[:, 4 * me:4 * me + 4], Copy))
+    done("s", S.activation(T.cmpb[:, 1024 + 193:2048:512], T.ut[:, 8:10], Copy))
+    for a in (0, 272):
+        tsw = done("s", S.activation(T.swb[:, a:a + 272], T.ut[:, 8:280], Copy))
     t = done("v", V.transpose(T.ltr[:, 64:96], T.lsrc[:, 64:96]))
-    done("v", V.memset(T.rz[:, 16:32], 0.0))
-    need("v", t, ("arc", sum(len(lanes(s)[2].get(me, ())) for s in range(N))))
-    t = done("v", V.tensor_copy(T.rya[:, 2 * LAND[me]:2 * LAND[me] + 2], T.yaa[:, 2 * me:2 * me + 2]))
-    done("v", V.memset(T.cmpb[:, 1024 + 193:2048:512], 0.0))
-    done("v", V.tensor_scalar(T.lc[:, 2:3], T.ltr[:, 64:65], 0.125, 32.0, MUL, MIN))
+    need("v", town)
+    tg = done("v", V.tensor_tensor(T.rg[:], T.rya[:, 0:32:2], T.rya[:, 1:32:2], ADD))
     need("v", t)
-    need("v", done("v", V.tensor_tensor(T.rh[:], T.rya[H[0], :], T.rya[H[1], :], ADD)))
+    done("v", V.tensor_scalar(T.lc[:, 2:3], T.ltr[:, 64:65], 0.125, 32.0, MUL, MIN))
+    need("v", tg)
+    need("v", done("v", V.tensor_tensor(T.rh[:], T.rg[H[0], :], T.rg[H[1], :], ADD)))
     need("v", done("v", V.tensor_tensor(T.rz[:, 0:16], T.rh[Q[0], :], T.rh[Q[1], :], ADD)))
     need("y", done("v", V.transpose(T.colt[:], T.rz[:])), tcr)
-    done("v", V.memset(T.swb[:], 0.0))
     for r in range(64, 128, 16):
         tdr = dma("dr", Y.dma_start(T.cr[r:r + 1, :], T.colt[0:16, :]))
 
     def landed(ranks):
-        return sum(len(eng.get(me, ())) for s in ranks for _k, eng in lanes(s)[1])
+        return sum(len(eng.get(me, ())) for s in ranks for _k, eng in lanes(s)[0])
 
     SA, SB, OWN = T.ps2, T.ps3, (T.ps4, T.ps5)
 
     def ownb(c, r=slice(0, 128)):
         return OWN[c][r, 0:1] if c < 2 else T.sbb[r, 32 * (c % 2):32 * (c % 2) + 1]
 
-    tok = {"R1": row(SB, T.landq, T.landp, 256, 512, ("arb", landed(range(N // 2, N))), ov, osc)}
-    tok["run"] = trun
-    tok["R0"] = row(SA, T.landq, T.landp, 0, 256, ("ara", landed(range(N // 2))))
+    tok = {"R1": row(SB, T.landq, T.landp, 256, 512, ("arb", landed(sides(me)[1])))}
+    tok["run"], tok["zero"] = trun, tsw
+    tok["R0"] = row(SA, T.landq, T.landp, 0, 256, ("ara", landed(sides(me)[0])), ov, osc)
     for c in range(2):
         a, b = 128 * c, 128 * c + 128
         tok["O%d" % c] = done("t", P.matmul_mx(OWN[c][:, 0:128], T.landq[:, a:b], T.landp[:, a:b], T.uq[:], T.up[:], True, True))

from concourse.bass import DstId, RemoteDMATransfer
from concourse.mybir import dt, AluOpType, ActivationFunctionType

F32, BF, I32, U16 = "float32", "bfloat16", "int32", "uint16"
CODE, PLANE = "float8_e4m3fn_x4", "uint8"
SCRATCH = {
    "ut": ("sbuf", [128, 512], BF),
    "xt": ("sbuf", [128, 2048], BF), "wt": ("sbuf", [128, 2048], BF),
    "uq": ("sbuf", [128, 128], CODE), "up": ("sbuf", [128, 128], PLANE),
    "urq": ("sbuf", [128, 128], CODE), "urp": ("sbuf", [128, 128], PLANE),
    "xq": ("sbuf", [128, 512], CODE), "xp": ("sbuf", [128, 512], PLANE),
    "wq": ("sbuf", [128, 512], CODE), "wp": ("sbuf", [128, 512], PLANE),
    "slotq": ("sbuf", [128, 512], CODE), "slotp": ("sbuf", [128, 512], PLANE),
    "landq": ("sbuf", [128, 512], CODE), "landp": ("sbuf", [128, 512], PLANE),
    "finq": ("sbuf", [128, 512], CODE), "finp": ("sbuf", [128, 512], PLANE),
    "zoff": ("sbuf", [128, 8], U16), "colidx": ("sbuf", [128, 128], F32),
    "mk": ("sbuf", [128, 128], F32),
    "lsrc": ("sbuf", [128, 128], F32), "ltr": ("sbuf", [128, 128], F32), "lc": ("sbuf", [128, 4], U16),
    "inrun": ("sbuf", [128, 1], F32),
    "dl": ("sbuf", [128, 4], F32), "thr": ("sbuf", [128, 512], F32),
    "colt": ("sbuf", [32, 32], BF), "yc": ("sbuf", [128, 32], BF), "rya": ("sbuf", [128, 32], BF), "rg": ("sbuf", [128, 16], BF),
    "rh": ("sbuf", [64, 16], BF), "rz": ("sbuf", [32, 32], BF),
    "cr": ("sbuf", [128, 512], BF), "idb": ("sbuf", [128, 128], F32), "yb": ("sbuf", [128, 512], F32),
}
for _k in "ab":
    for _n, _w, _d in (("sa", 64, F32), ("sb", 64, F32), ("cmp", 2048, BF), ("vals", 64, BF),
                       ("rel", 512, BF), ("sgn", 512, BF), ("nlt", 8, F32), ("so", 1024, BF),
                       ("pl", 4, U16), ("sw", 544, BF), ("tr", 1056, BF), ("ya", 48, BF),
                       ("za", 48, BF), ("zb", 48, BF), ("uu", 48, BF), ("off", 48, U16)):
        SCRATCH[_n + _k] = ("sbuf", [128, _w], _d)
for _k in range(8):
    SCRATCH["ps%d" % _k] = ("psum", [128, 512], F32)

SEMAPHORES = ["cv", "cs", "ct", "cg", "du", "dx0", "dx1", "dx2", "dw", "dr", "dy", "di",
              "ara", "arb", "arc", "ls"]

PLAN = {"a": "vT0 sd0 vq1 st0 vn0 vn1 st1 vi0 vT1 vi1 sd1 vx0 sr3 vx1 st2 vn2 vn3 st3 vx2 vi2 ss3 vz0 vi3 vz1 vz2 vz3",
        "b": "vT1 vA2 vA3 sr2 sr3 vB2 vB3 vx0 vx1 ss2 ss3 vA0 vA1 vz2 vB0 vB1 vz3 vz0 vz1"}


def rank_program(g, core, T, topo):
    me = T.rank_of(core)
    if me is None:
        return
    V, S, P, Y = g.vector, g.scalar, g.tensor, g.sync
    AF = ActivationFunctionType
    Copy, Ident = AF.Copy, AF.Identity
    GT, GE, LT = AluOpType.is_gt, AluOpType.is_ge, AluOpType.is_lt
    ADD, MUL, MIN = AluOpType.add, AluOpType.mult, AluOpType.min
    cnt, seen = {}, {}
    queue = {"v": V, "s": S, "t": P, "g": g, "y": Y}
    CORES = T.cores
    N = len(CORES)
    CH = 512 // N
    H = (slice(0, 64), slice(64, 128))
    Q = [slice(32 * a, 32 * a + 32) for a in range(4)]

    def sides(s):
        home = [d for d in range(N) if topo.die(CORES[d]) == topo.die(CORES[s])]
        return home, [d for d in range(N) if d not in home]

    def land(s, d):
        home, far = sides(d)
        return home.index(s) if s in home else (4, 6, 5, 7)[far.index(s)]

    flip = sides(me)[1][0] < me

    def need(q, *toks):
        for sem, val in toks:
            if seen.get((q, sem), 0) < val:
                queue[q].wait_ge(T.sem[sem], val)
                seen[(q, sem)] = val

    def done(q, inst):
        sem = "c" + q
        inst.then_inc(T.sem[sem], 1)
        cnt[sem] = cnt.get(sem, 0) + 1
        return (sem, cnt[sem])

    def dma(sem, inst):
        inst.then_inc(T.sem[sem], 16)
        cnt[sem] = cnt.get(sem, 0) + 16
        return (sem, cnt[sem])

    def iota(out, pattern, base, step, alone=False):
        if alone:
            need("g", ("cg", cnt["cg"]))
        return done("g", g.iota(out, pattern, base, step, allow_small_or_imprecise_dtypes=True))

    tu = dma("du", Y.dma_start(T.ut[:, 0:8], T.u[:, 0:8]))
    tx = [dma("dx0", S.dma_start(T.xt[:, 0:512], T.x[:, 0:512])),
          dma("dx1", Y.dma_start(T.xt[:, 512:1024], T.x[:, 512:1024])),
          dma("dx2", S.dma_start(T.xt[:, 1024:2048], T.x[:, 1024:2048]))]
    need("y", *tx)
    dma("dw", Y.dma_start(T.wt[:, 0:1024], T.w[:, 0:1024]))
    tw = dma("dw", Y.dma_start(T.wt[:, 1024:2048], T.w[:, 1024:2048]))

    tps = iota(T.lsrc[:, 96:128], [[128, 32]], 0, 1)
    tci = iota(T.colidx[:], [[32, 128]], 0, 0)
    for m in range(2):
        iota(T.lsrc[:, 32 * m:32 * m + 16], [[8, 8], [136, 2]], 64 * m, 0)
        tls = iota(T.lsrc[:, 32 * m + 16:32 * m + 32], [[8, 8], [-128, 2]], 128 + 64 * m, 0)
    iota(T.valsb[:, 0:32], [[128, 2], [1, 16]], -256, 1)
    for a in range(4):
        tva = iota(T.valsa[Q[a], :], [[128, 4], [4, 16]], a - 256, 4, True)
    for r in H:
        iota(T.lsrc[r, 64:80], [[8, 8], [136, 2]], 0, 2, True)
        iota(T.lsrc[r, 80:96], [[8, 8], [-128, 2]], 128 + 32, 2, True)
    for a in range(4):
        tvb = iota(T.valsb[Q[a], 32:64], [[64, 2], [2, 16]], 128 * (a // 2) + a % 2, 2, True)

    done("v", V.memset(T.ut[:, 8:512], 0.0))
    tz = done("v", V.memset(T.zoff[:], 0))
    done("v", V.memset(T.swa[:], 0.0))

    need("v", tu, tz)
    tq = done("v", V.quantize_mx(T.uq[:], T.up[:], T.ut[:]))
    need("v", tps)
    tps = done("v", V.transpose(T.ltr[:, 96:128], T.lsrc[:, 96:128]))
    need("v", tq)
    tur = done("v", V.tensor_copy(T.urq[:].bitcast(dt.uint32), T.uq[:].bitcast(dt.uint32).indirect(T.zoff[:])))
    need("s", tq, tz)
    tup = done("s", S.activation(T.urp[:], T.up[:].indirect(T.zoff[:]), Copy))

    def row(ps, q, p, a, b, *toks):
        need("t", tur, tup, *toks)
        return done("t", P.matmul_mx(ps[:, 0:b - a], T.urq[:], T.urp[:], q[:, a:b], p[:, a:b], True, True))

    def count(k, R, own, tok, second=None):
        cm, so, rel, sgn, nlt = [T[n + k] for n in ("cmp", "so", "rel", "sgn", "nlt")]
        plan = PLAN[k].split()
        tok = dict(tok)
        turn = int(k == "b" and flip)
        bank = {}

        def emit(q, w, c):
            h, at, o = c // 2, 512 * c, 256 * (c % 2)
            late = c % 2
            if w == "q":
                tk = second()
                need(q, tok["T0"])
                done("v", V.tensor_scalar(T.lc[:, 0:2], T.ltr[:, 0:64:32], 0.125, None, MUL))
                return tk
            deps = {"T": ["R%d" % c], "d": ["T%d" % c], "t": ["d%d" % h], "i": ["t%d" % c], "n": ["T%d" % h],
                    "A": ["O%d" % c, "R%d" % h], "B": ["A%d" % c], "x": ["O%d" % c, "R%d" % (1 - h)], "r": ["O%d" % c, "R0"],
                    "s": ["r%d" % c], "z": [x for x in tok if x in ("run", "zero") or x[0] in "inBxs" and x[1:] == str(c)]}[w]
            b = {"T": c, "i": h, "n": h, "A": h, "B": h, "x": 1 - h, "r": 1 - h}.get(w)
            need(q, *[tok[x] for x in deps])
            need(q, *[t for (bb, qq), t in bank.items() if bb == b and qq != q])
            if w == "T":
                for a in range(4):
                    src = R[c][Q[a], a:256:4] if k == "a" else R[c][Q[a], 128 * (a // 2) + a % 2:128 * (a // 2) + 128:2]
                    tk = done("v", V.transpose(T[("sa", "sb")[c] + k][Q[a], 0:64], src))
                tok["O%d" % (2 * c)] = tok["O%d" % (2 * c + 1)] = tk
            elif w == "d":
                tk = done("s", S.activation(T.dl[:, 2 * c:2 * c + 2], T[("sa", "sb")[c] + k][:, 0:64:32], AF.Abs,
                                            bias=2.0 ** -120, scale=0.6 * 2.0 ** -23))
            elif w == "t":
                need(q, tmk)
                to = T.thr[:, 128 * c:128 * c + 128]
                if q == "s":
                    tk = done("s", S.activation(to, T.mk[:], Ident, bias=own(c), scale=T.dl[:, c:c + 1]))
                else:
                    tk = done("v", V.tensor_scalar(to, T.mk[:], T.dl[:, c:c + 1], own(c), MUL, ADD))
            elif w == "i":
                tk = done("v", V.tensor_tensor(cm[:, at:at + 128], R[h][:, 128 * late:128 * late + 128],
                                               T.thr[:, 128 * c:128 * c + 128], GT))
            elif w == "n":
                tk = done("v", V.tensor_scalar(cm[:, at + 128:at + 256], R[h][:, 128 - 128 * late:256 - 128 * late], own(c), None,
                                               (GT, GE)[late]))
            elif w == "A":
                tk = done("v", V.tensor_scalar(cm[:, at + h:at + h + 192], R[h][:, 64 - 64 * late:256 - 64 * late], own(c), None,
                                               (GT, GE)[late]))
            elif w == "B":
                r, to = H[1 - late], at + h + (64 if h else 128 * late)
                tk = done("v", V.tensor_scalar(cm[r, to:to + 64], R[h][r, 192 * late:192 * late + 64], own(c, r), None,
                                               (GE, GT)[late]))
            elif w == "x":
                n = 256 if k == "a" else 192
                tk = done("v", V.tensor_scalar(cm[:, at + n:at + n + 256], R[1 - h][:, 0:256], own(c), None, (GT, GE)[h ^ turn]))
            elif w == "r":
                tk = done("s", S.activation(rel[:, o:o + 256], R[0][:, 0:256], (AF.Relu, AF.Sign)[turn], bias=own(c), scale=-1.0))
            elif w == "s":
                tk = done("s", S.activation(sgn[:, o:o + 256], rel[:, o:o + 256], (AF.Sign, AF.Relu)[turn], scale=-1.0,
                                            accum_out=nlt[:, 4 * late:4 * late + 1]))
            else:
                across = "x%d" % c in tok
                n = ((128, 256), (97, 224))[k == "b"][across]
                first = (-256.0 if k == "a" else T.inrun[:]) if across else nlt[:, 4 * late:4 * late + 1]
                tk = done("v", V.tensor_tensor_scan(so[:, 256 * c + 256 - n:256 * c + 256], cm[:, at:at + n], cm[:, at + n:at + 2 * n],
                                                    first, ADD, ADD))
            if b is not None:
                bank[(b, q)] = tk
            return tk

        for x in plan:
            tok["R1" if x[1] == "q" else x[1:]] = tk = emit(x[0], x[1], int(x[2]))
        return tk

    def make_list(k, n, *tok):
        pl, sw, tr, ya, za, zb, uu, off = [T[x + k] for x in ("pl", "sw", "tr", "ya", "za", "zb", "uu", "off")]
        need("v", *tok)
        tk = done("v", V.tensor_scalar(pl[:], T["so" + k][:, 255:1024:256], 256.0, None, ADD))
        need("v", tk)
        tk = done("v", V.tensor_copy(sw[:, 16:528].indirect(pl[:]), T["vals" + k][:]))
        need("v", tk)
        t0 = done("v", V.transpose(tr[:, 0:512], sw[:, 16:528]))
        tk = done("v", V.transpose(tr[:, 512:1056], sw[:]))
        need("v", tk)
        tk = done("v", V.tensor_tensor(ya[:, 0:33], tr[:, 0:1056:32], tr[:, 16:1056:32], ADD))
        need("v", tk)
        done("v", V.tensor_tensor(za[H[0], 0:33], ya[H[0], 0:33], ya[H[1], 0:33], ADD))
        for a in range(2):
            tk = done("v", V.tensor_tensor(zb[Q[a], 0:33], ya[Q[a ^ 1], 0:33], ya[Q[a ^ 3], 0:33], ADD))
        need("v", tk)
        for r in H:
            tk = done("v", V.tensor_tensor(uu[r, 0:33], za[H[0], 0:33], zb[H[0], 0:33], ADD))
        need("v", tk)
        return t0, done("v", V.tensor_scalar(off[:, 0:16 * n], uu[:, 0:33].indirect(T.lc[:, 0:n]), 256.0, None, ADD))

    RA, RB = T.ps0, T.ps1

    def quant(i):
        need("v", tx[i])
        a, b = (0, 128, 256, 512)[i:i + 2]
        return done("v", V.quantize_mx(T.xq[:, a:b], T.xp[:, a:b], T.xt[:, 4 * a:4 * b]))

    def owna(c):
        return (T.saa, T.sba)[c // 2][:, 32 * (c % 2):32 * (c % 2) + 1]

    quant(0)
    tra = row(RA, T.xq, T.xp, 0, 256, quant(1))
    need("v", tci, tps)
    tmk = done("v", V.tensor_scalar(T.mk[:], T.colidx[:], T.ltr[:, 96:97], -1.0, LT, MUL))
    need("v", tls)
    done("v", V.transpose(T.ltr[:, 0:64], T.lsrc[:, 0:64]))
    tcount = count("a", (RA, RB), owna, {"R0": tra}, lambda: row(RB, T.xq, T.xp, 256, 512, quant(2)))
    t, tof = make_list("a", 2, tcount, tva)
    need("s", t)
    tya = done("s", S.activation(T.yc[:], T.tra[:, 0:512:16], Copy))

    need("v", tof)
    need("s", tof)

    def codes(dst, at, src, off, a, b):
        return done("v", V.tensor_copy(dst[:, at:at + b - a].bitcast(dt.uint32), src[:].bitcast(dt.uint32).indirect(off[:, a // 16:b // 16])))

    def scales(dst, at, src, off, a, b, q="s"):
        to, win = dst[:, at:at + b - a], src[:].indirect(off[:, a // 16:b // 16])
        return done(q, S.activation(to, win, Copy) if q == "s" else V.tensor_copy(to, win))

    def lanes(s):
        home, far = sides(s)
        near = [d for d in home if d != s]
        el = topo.engines(CORES[s], CORES[far[0]])
        ev, od = el[0::2], el[1::2]
        four = {d: el[4 * i:4 * i + 4] for i, d in enumerate(far)}
        calls = [("q", four), ("p", four), ("q", dict(zip(near, (od[:4], od[4:], ev)))),
                 ("p", dict(zip(near, (ev[:4], ev[4:], od))))]
        return calls, dict(zip(far + near, (ev[0:2], ev[2:4], ev[4:6], ev[6:8], od[0:2], od[2:4], od[4:8])))

    calls, allq = lanes(me)
    picked = []
    for kind, eng in calls:
        a, b = CH * min(eng), CH * max(eng) + CH
        picked.append((codes(T.slotq, a, T.xq, T.offa, a, b) if kind == "q" else scales(T.slotp, a, T.xp, T.offa, a, b)))
    ov = codes(T.landq, CH * land(me, me), T.xq, T.offa, CH * me, CH * me + CH)
    osc = scales(T.landp, CH * land(me, me), T.xp, T.offa, CH * me, CH * me + CH)

    def send(eng, src, dst, w, sem=None):
        tl = []
        for d in eng:
            rid, pid, _s = topo.addr(CORES[d])
            a, b = src[:, w * d:w * d + w], dst[:, w * land(me, d):w * land(me, d) + w]
            if src.name == "slotq":
                a, b = a.bitcast(dt.uint8), b.bitcast(dt.uint8)
            tl.append(RemoteDMATransfer(dst_ids=[DstId(rid=rid, pnc=pid)], dma_engine_mask=sum(1 << e for e in eng[d]),
                                        remote_sem=T.sem[sem or ("ara" if d in sides(me)[0] else "arb")], src=a, dst=b))
            cnt["ls"] = cnt.get("ls", 0) + len(eng[d])
        g.remote_dma_fused(tl, local_sem=T.sem.ls)

    need("g", tya)
    send(allq, T.yc, T.rya, 4, "arc")
    for (kind, eng), tk in zip(calls, picked):
        need("g", tk)
        send(eng, T["slot" + kind], T["land" + kind], CH)
    for a in range(4):
        iota(T.cmpb[Q[a], 1024:2048:512], [[0, 2]], a % 2 - 256 * flip, 2, True)
    for r in H:
        trun = iota(T.inrun[r, :], [[1, 1]], -256, 1, True)
    iota(T.cr[:, 0:256], [[1, 4], [0, CH]], sides(me)[0][0] - 256, 0, True)
    tcr = iota(T.cr[:, 256:512], [[1, 2], [2, 2], [0, CH]], sides(me)[1][0] - 256, 0)

    need("v", tw, tvb)
    twq = done("v", V.quantize_mx(T.wq[:], T.wp[:], T.wt[:]))
    need("s", tya, ("arc", sum(len(lanes(s)[1].get(me, ())) for s in range(N))))
    done("s", S.activation(T.rz[:, 16:32], T.ut[Q[0], 8:24], Copy))
    town = done("s", S.activation(T.rya[:, 4 * land(me, me):4 * land(me, me) + 4], T.yc[:, 4 * me:4 * me + 4], Copy))
    done("s", S.activation(T.cmpb[:, 1024 + 193:2048:512], T.ut[:, 8:10], Copy))
    for a in (0, 272):
        tsw = done("s", S.activation(T.swb[:, a:a + 272], T.ut[:, 8:280], Copy))
    t = done("v", V.transpose(T.ltr[:, 64:96], T.lsrc[:, 64:96]))
    need("v", town)
    tg = done("v", V.tensor_tensor(T.rg[:], T.rya[:, 0:32:2], T.rya[:, 1:32:2], ADD))
    need("v", t)
    done("v", V.tensor_scalar(T.lc[:, 2:3], T.ltr[:, 64:65], 0.125, 32.0, MUL, MIN))
    need("v", tg)
    need("v", done("v", V.tensor_tensor(T.rh[:], T.rg[H[0], :], T.rg[H[1], :], ADD)))
    need("v", done("v", V.tensor_tensor(T.rz[:, 0:16], T.rh[Q[0], :], T.rh[Q[1], :], ADD)))
    need("y", done("v", V.transpose(T.colt[:], T.rz[:])), tcr)
    for r in range(64, 128, 16):
        tdr = dma("dr", Y.dma_start(T.cr[r:r + 1, :], T.colt[0:16, :]))

    def landed(ranks):
        return sum(len(eng.get(me, ())) for s in ranks for _k, eng in lanes(s)[0])

    SA, SB, OWN = T.ps2, T.ps3, (T.ps4, T.ps5)

    def ownb(c, r=slice(0, 128)):
        return OWN[c][r, 0:1] if c < 2 else T.sbb[r, 32 * (c % 2):32 * (c % 2) + 1]

    tok = {"R1": row(SB, T.landq, T.landp, 256, 512, ("arb", landed(sides(me)[1])))}
    tok["run"], tok["zero"] = trun, tsw
    tok["R0"] = row(SA, T.landq, T.landp, 0, 256, ("ara", landed(sides(me)[0])), ov, osc)
    for c in range(2):
        a, b = 128 * c, 128 * c + 128
        tok["O%d" % c] = done("t", P.matmul_mx(OWN[c][:, 0:128], T.landq[:, a:b], T.landp[:, a:b], T.uq[:], T.up[:], True, True))
    _t, tof = make_list("b", 3, count("b", (SA, SB), ownb, tok))

    need("v", tof)
    need("s", tof)
    YP = (T.ps6, T.ps7, T.ps0, T.ps1)
    ty = []
    for k in range(4):
        a, b = 128 * k, 128 * k + 128
        if k % 2 == 0:
            tv = codes(T.finq, a, T.landq, T.offb, a, a + 256)
            ts = scales(T.finp, a, T.landp, T.offb, a, a + 256)
        need("t", twq, tv, ts)
        ty.append(done("t", P.matmul_mx(YP[k][:, 0:128], T.wq[:, a:b], T.wp[:, a:b], T.finq[:, a:b], T.finp[:, a:b], True, True)))
    need("s", tdr)
    ti = done("s", S.activation(T.idb[:], T.cr[:].indirect(T.offb[:, 32:40]), Ident, bias=256.0))
    tc = []
    for b, q in enumerate("vvsv"):
        need(q, ty[b])
        to, src = T.yb[:, 128 * b:128 * b + 128], YP[b][:, 0:128]
        tc.append(done(q, V.tensor_copy(to, src) if q == "v" else S.activation(to, src, Copy)))
    need("y", ti)
    dma("di", Y.dma_start(T.ids[:], T.idb[0:128:16, :]))
    for q, a in (("y", 0), ("s", 2)):
        need(q, *tc[a:a + 2])
        dma("dy", queue[q].dma_start(T.y[:, 128 * a:128 * a + 256], T.yb[:, 128 * a:128 * a + 256]))

    for sem in ("cg", "ls", "dw", "ct", "cv", "cs", "di", "dy"):
        need("g", (sem, cnt[sem]))
